import numpy as np
import ml_dtypes


def mxq(x, axis, fmt="e4m3"):
    dtype, down = {"e4m3": (ml_dtypes.float8_e4m3fn, 7), "e5m2": (ml_dtypes.float8_e5m2, 14)}[fmt]
    v = np.moveaxis(np.asarray(x, np.float32).astype(ml_dtypes.bfloat16).astype(np.float64), axis, -1)
    blocks = v.reshape(v.shape[:-1] + (-1, 32))
    amax = np.abs(blocks).max(-1, keepdims=True)
    byte = np.maximum(np.where(amax > 0, np.frexp(amax)[1] - 1 + 127, 0) - down, 1)
    scale = np.exp2(byte - 127.0)
    codes = (blocks / scale).astype(np.float32).astype(dtype).astype(np.float64)
    return np.moveaxis((codes * scale).reshape(v.shape), -1, axis)


WIDE = False


def mx_kscale(k):
    if not WIDE:
        return np.ones(k)
    levels = np.array([10, -10, 5, -5, 0])
    if k % 512:
        return np.exp2(np.random.permutation(np.resize(levels, k // 32))).repeat(32)
    a = np.empty((k // 512, 16))
    for p in range(k // 512):
        a[p, :8] = np.random.permutation(np.resize(levels, 8))
        for g in range(8):
            far = levels[np.abs(levels - a[p, g]) >= 10]
            a[p, g + 8] = far[np.random.randint(len(far))]
    return np.exp2(a.ravel()).repeat(32)


def f64(x):
    return np.asarray(x).astype(np.float64)


def striped(idx):
    return np.tile(idx.reshape(-1, 16).T, (8, 1)).astype(np.uint16)


def unstriped(offs):
    return offs[:16].T.reshape(-1).astype(np.int64)


def pack_weight(w):
    k, n = w.shape
    w = f64(np.asarray(w, np.float32).astype(ml_dtypes.bfloat16)).reshape(k // 32, 32, n)
    amax = np.abs(w).max(1)
    byte = np.clip(np.where(amax > 0, np.frexp(amax)[1] - 1 + 127 - 7, 1), 1, 254)
    scaled = (w * np.exp2(127.0 - byte)[:, None, :]).reshape(k, n).astype(np.float32)
    words = np.ascontiguousarray(scaled.reshape(k // 512, 128, 4, n).transpose(0, 1, 3, 2)).astype(ml_dtypes.float8_e4m3fn).view(np.uint8)
    return words, np.ascontiguousarray(byte.astype(np.uint8).reshape(k // 512, 16, n))


def unpack_weight(words, scales):
    g, p, n, _ = words.shape
    vals = np.ascontiguousarray(words).view(ml_dtypes.float8_e4m3fn).astype(np.float64) * np.repeat(np.exp2(scales.astype(np.float64) - 127.0), 8, axis=1)[..., None]
    return vals.transpose(0, 1, 3, 2).reshape(g * 512, n)


K, T, S, V = 1024, 2048, 512, 512
P = 2 ** 7


def setup_inputs():
    n = np.random.standard_normal
    s = mx_kscale(K)[:, None]
    packed_xT = pack_weight(n((K, T)) * s)
    return {
        "x_words": packed_xT[0],
        "x_scales": packed_xT[1],
        "hT": (n((K, V)) / np.sqrt(K) / s).astype(np.float32),
        "norm": (np.tile(np.random.uniform(0.0, 1.0, T), (P, 1))).astype(np.float32),
        "post": (np.random.uniform(0.0, 1.0, (V, S))).astype(np.float32),
        "haz": (np.tile(np.random.uniform(0.01, 0.2, S), (P, 1))).astype(np.float32),
        "start": (np.tile((np.arange(S) == 0) * 1.0 + np.random.uniform(0.0, 0.001, S), (P, 1))).astype(np.float32),
        "offs": striped(np.random.permutation(T)[:S]),
    }


def reference(x_words, x_scales, hT, norm, post, haz, start, offs):
    hTq = mxq(f64(hT), 0, "e4m3")
    xq = unpack_weight(x_words, x_scales)[:, unstriped(offs)]
    y = (hTq.T @ xq) - (f64(norm)[:1][:, unstriped(offs)])
    jt = f64(post) * np.exp(0.7 * y)
    ch = jt * f64(haz)[:1]
    gr = jt - ch
    c0 = ch.sum(axis=1, keepdims=True)
    nw = np.pad(gr, ((0, 0), (1, 0)))[:, :S] + f64(start)[:1] * c0
    ev = nw.sum(axis=1, keepdims=True)
    return 100.0 * (nw / ev)

@@ -1,0 +1,206 @@
+from contextlib import ExitStack
+
+import concourse.mybir as mybir
+from concourse.masks import make_identity
+
+K, T, S, V = 1024, 2048, 512, 512
+P = 128
+PASSES = 2
+NB = 4
+FLOPS = 2 * K * S * V
+
+F32 = mybir.dt.float32
+BF16 = mybir.dt.bfloat16
+I32 = mybir.dt.int32
+U32 = mybir.dt.uint32
+U16 = mybir.dt.uint16
+U8 = mybir.dt.uint8
+FP8X4 = mybir.dt.float8_e4m3fn_x4
+ALU = mybir.AluOpType
+ACT = mybir.ActivationFunctionType
+
+W = 256
+NROW = 16
+
+
+def tile_picked_ybocpd_post_p_kernel(tc, x_words, x_scales, hT, norm, post, haz, start, offs, out):
+    nc = tc.nc
+    with ExitStack() as ctx:
+        keep = ctx.enter_context(tc.tile_pool(name="keep", bufs=1))
+        psum = ctx.enter_context(tc.psum_pool(name="psum", bufs=1))
+
+        offsets = keep.tile([P, S // 16], U16, name="offsets")
+        nc.sync.dma_start(offsets[:], offs)
+
+        h_raw = {}
+        post_sb = {}
+        x_win = {}
+
+        def load_h(c, g, dst):
+            h_raw[c, g] = dst.rearrange("p (j w) -> p j w", j=4)
+            nc.sync.dma_start(out=h_raw[c, g],
+                              in_=hT[512 * g:512 * (g + 1), c * W:(c + 1) * W].rearrange("(p j) w -> p j w", j=4))
+
+        def load_post(b, dst):
+            post_sb[b] = dst
+            nc.sync.dma_start(out=dst, in_=post[b * P:(b + 1) * P, :])
+
+        def load_x(g, dst):
+            x_win[g] = dst
+            nc.sync.dma_start(out=dst, in_=x_words[g].rearrange("p n t -> p (n t)").bitcast(I32))
+
+        grown = keep.tile([P, NB, S], F32, name="grown")
+        nc.gpsimd.memset(grown[:, :, 0:1], 0.0)
+        s_win = keep.tile([P, T], U8, name="s_win", align_bytes=64)
+        nc.gpsimd.memset(s_win[:].bitcast(I32), 0)
+        n_win = keep.tile([P, T], F32, name="n_win", align_bytes=64)
+        nc.vector.memset(n_win[:], 0.0)
+        hs_rows = keep.tile([P, P], F32, name="hs_rows")
+        nc.gpsimd.dma_start(out=hs_rows[0:64, :], in_=haz[0:16, :].rearrange("r (b p) -> (r b) p", p=P))
+        nc.gpsimd.dma_start(out=hs_rows[64:128, :], in_=start[0:16, :].rearrange("r (b p) -> (r b) p", p=P))
+        load_h(0, 0, keep.tile([P, 4 * W], F32, name="h_raw00", tag="slot_b", align_bytes=64)[:])
+        for q in range(4):
+            nc.sync.dma_start(out=s_win[32 * q:32 * q + 8, :].bitcast(I32),
+                              in_=x_scales[:, 4 * q:4 * q + 4, :].bitcast(I32))
+        nc.sync.dma_start(out=n_win[NROW:NROW + 1, :], in_=norm[0:1, :])
+        load_h(0, 1, keep.tile([P, 4 * W], F32, name="h_raw01", tag="slot_c", align_bytes=64)[:])
+
+        ident = keep.tile([P, P], F32, name="ident")
+        make_identity(nc, ident[:])
+
+        warm = keep.tile([P, 1], F32, name="warm", tag="slot_a", align_bytes=64)
+        nc.scalar.activation(out=warm[:], in_=grown[:, 0, 0:1], func=ACT.Exp)
+        x_all = keep.tile([P, PASSES * T], I32, name="x_all", tag="slot_a", align_bytes=64)
+        load_x(0, x_all[:, 0:T])
+        load_x(1, x_all[:, T:2 * T])
+
+        h_bf, h_codes, h_scales = {}, {}, {}
+
+        def cast_h(c, g, eng):
+            h_bf[c, g] = keep.tile([P, W, 4], BF16, name="h_bf%d%d" % (c, g), tag="h_bf%d%d" % (c, g), align_bytes=64)
+            dst = h_bf[c, g][:].rearrange("p (c i) t -> p c t i", i=4)
+            srcv = h_raw[c, g].rearrange("p t (c i) -> p c t i", i=4)
+            if eng == "s":
+                nc.scalar.copy(out=dst, in_=srcv)
+            else:
+                nc.vector.tensor_copy(out=dst, in_=srcv)
+
+        def quant_h(c, g):
+            h_codes[c, g] = keep.tile([P, W], U32, name="h_codes%d%d" % (c, g), align_bytes=64)
+            h_scales[c, g] = keep.tile([P, W], U8, name="h_scales%d%d" % (c, g), align_bytes=64)
+            nc.vector.quantize_mx(out=h_codes[c, g][:].bitcast(FP8X4), scales=h_scales[c, g][:],
+                                  in_=h_bf[c, g][:].rearrange("p w j -> p (w j)"))
+
+        cast_h(0, 0, "s")
+        load_h(1, 0, keep.tile([P, 4 * W], F32, name="h_raw10", tag="slot_b", align_bytes=64)[:])
+        cast_h(0, 1, "s")
+        load_post(0, keep.tile([P, S], F32, name="post0", tag="slot_c", align_bytes=64)[:])
+
+        n_pick = keep.tile([P, S], F32, name="n_pick")
+        nc.vector.tensor_scalar(n_pick[:], n_win[:].indirect(offsets[:]), -0.7, 0.0, ALU.mult, ALU.add)
+        n_ps = psum.tile([P, NB, P], F32, name="n_ps", tag="e", bufs=2)
+        for jb in range(NB):
+            nc.tensor.transpose(n_ps[:, jb, :], n_pick[:, jb * P:(jb + 1) * P], ident[:])
+        bias = keep.tile([P, NB], F32, name="bias")
+        nc.vector.tensor_copy(out=bias[:], in_=n_ps[:, :, NROW])
+
+        hs_ps = psum.tile([P, P], F32, name="hs_ps", tag="e", bufs=2)
+        nc.tensor.transpose(hs_ps[:], hs_rows[:], ident[:])
+        hs_cols = keep.tile([P, 2, NB], F32, name="hs_cols")
+        nc.vector.tensor_copy(out=hs_cols[:], in_=hs_ps[:].rearrange("p (a r) -> p a r", a=2)[:, :, 0:NB])
+        haz_ps = psum.tile([P, S], F32, name="haz_ps")
+        start_ps = psum.tile([P, S], F32, name="start_ps")
+        for a, bank in enumerate((haz_ps, start_ps)):
+            for jb in range(NB):
+                nc.tensor.transpose(bank[:, jb * P:(jb + 1) * P], hs_cols[:, a, jb:jb + 1].to_broadcast([P, P]), ident[:])
+        stay = keep.tile([P, S], F32, name="stay")
+        nc.scalar.activation(out=stay[:], in_=haz_ps[:], func=ACT.Copy, scale=-1.0, bias=1.0)
+
+        quant_h(0, 0)
+        s_pick = keep.tile([P, S], U8, name="s_pick", align_bytes=64)
+        nc.vector.tensor_copy(s_pick[:], s_win[:].indirect(offsets[:]))
+        quant_h(0, 1)
+        late = keep.tile([P, 4 * W + 3 * S], F32, name="late", tag="h_bf01", align_bytes=64)
+        load_h(1, 1, late[:, 0:4 * W])
+        for b in range(1, NB):
+            load_post(b, late[:, 4 * W + (b - 1) * S:4 * W + b * S])
+        x_pick = [keep.tile([P, S], U32, name="x_pick%d" % g, align_bytes=64) for g in range(PASSES)]
+        nc.vector.tensor_copy(x_pick[0][:], x_win[0].bitcast(U32).indirect(offsets[:]))
+
+        sums = {}
+
+        def mx_pass(c, g, jb):
+            if g == 0:
+                sums[c, jb] = psum.tile([P, W], F32, name="sums%d%d" % (c, jb), tag="sums%d" % jb)
+            cols = slice(jb * P, (jb + 1) * P)
+            nc.tensor.matmul_mx(out=sums[c, jb][:], lhsT=x_pick[g][:, cols].bitcast(FP8X4),
+                                lhsT_scale=s_pick[4 * g:P, cols], rhs=h_codes[c, g][:].bitcast(FP8X4),
+                                rhs_scale=h_scales[c, g][:], start=(g == 0), stop=(g == PASSES - 1))
+
+        dens = keep.tile([P, NB, V], F32, name="dens")
+
+        def exp_of(c, jb):
+            nc.scalar.activation(out=dens[:, jb, c * W:(c + 1) * W], in_=sums[c, jb][:], func=ACT.Exp,
+                                 bias=bias[:, jb:jb + 1], scale=0.7)
+
+        for jb in range(NB):
+            mx_pass(0, 0, jb)
+        for half in range(2):
+            nc.vector.tensor_copy(x_pick[1][:, half * 256:(half + 1) * 256],
+                                  x_win[1].bitcast(U32).indirect(offsets[:, half * 16:(half + 1) * 16]))
+            for jb in (2 * half, 2 * half + 1):
+                mx_pass(0, 1, jb)
+                exp_of(0, jb)
+
+        joint = {}
+        stats = {}
+
+        def turn(b):
+            e_ps = psum.tile([P, S], F32, name="e_ps%d" % b, tag="e", bufs=2)
+            for jb in range(NB):
+                nc.tensor.transpose(e_ps[:, jb * P:(jb + 1) * P], dens[:, jb, b * P:(b + 1) * P], ident[:])
+            joint[b] = keep.tile([P, S], F32, name="joint%d" % b)
+            nc.vector.tensor_tensor(out=joint[b][:], in0=e_ps[:], in1=post_sb[b], op=ALU.mult)
+            nc.gpsimd.tensor_tensor(out=grown[:, b, 1:S], in0=joint[b][:, 0:S - 1], in1=stay[:, 0:S - 1], op=ALU.mult)
+
+        def change(b):
+            stats[b] = keep.tile([P, 4], F32, name="stats%d" % b)
+            ch = keep.tile([P, S], F32, name="ch", tag="ch", bufs=2)
+            nc.vector.scalar_tensor_tensor(out=ch[:], in0=haz_ps[:], scalar=1.0, in1=joint[b][:],
+                                           op0=ALU.mult, op1=ALU.mult, accum_out=stats[b][:, 0:1])
+
+        def finish(b, eng):
+            nw = keep.tile([P, S], F32, name="nw%d" % b)
+            nc.vector.scalar_tensor_tensor(out=nw[:], in0=start_ps[:], scalar=stats[b][:, 0:1], in1=grown[:, b, :],
+                                           op0=ALU.mult, op1=ALU.add, accum_out=stats[b][:, 1:2])
+            nc.vector.reciprocal(out=stats[b][:, 2:3], in_=stats[b][:, 1:2])
+            res = keep.tile([P, S], F32, name="res%d" % b)
+            if eng == "s":
+                nc.scalar.activation(out=stats[b][:, 3:4], in_=stats[b][:, 2:3], func=ACT.Copy, scale=100.0)
+                nc.scalar.activation(out=res[:], in_=nw[:], func=ACT.Copy, scale=stats[b][:, 3:4])
+            elif eng == "g":
+                nc.gpsimd.tensor_scalar(res[:], nw[:], stats[b][:, 2:3], 100.0, ALU.mult, ALU.mult)
+            else:
+                nc.vector.tensor_scalar(res[:], nw[:], stats[b][:, 2:3], 100.0, ALU.mult, ALU.mult)
+            nc.sync.dma_start(out=out[b * P:(b + 1) * P, :], in_=res[:])
+
+        cast_h(1, 0, "v")
+        quant_h(1, 0)
+        turn(0)
+        cast_h(1, 1, "s")
+        change(0)
+        turn(1)
+        quant_h(1, 1)
+        for jb in range(NB):
+            mx_pass(1, 0, jb)
+            mx_pass(1, 1, jb)
+            exp_of(1, jb)
+        finish(0, "s")
+        change(1)
+        finish(1, "s")
+        turn(2)
+        change(2)
+        turn(3)
+        finish(2, "s")
+        change(3)
+        finish(3, "v")

@@ -30,7 +30,6 @@ def tile_picked_ybocpd_post_p_kernel(tc, x_words, x_scales, hT, norm, post, haz,
         psum = ctx.enter_context(tc.psum_pool(name="psum", bufs=1))
 
         offsets = keep.tile([P, S // 16], U16, name="offsets")
-        nc.sync.dma_start(offsets[:], offs)
 
         h_raw = {}
         post_sb = {}
@@ -51,7 +50,7 @@ def tile_picked_ybocpd_post_p_kernel(tc, x_words, x_scales, hT, norm, post, haz,
 
         grown = keep.tile([P, NB, S], F32, name="grown")
         nc.gpsimd.memset(grown[:, :, 0:1], 0.0)
-        s_win = keep.tile([P, T], U8, name="s_win", align_bytes=64)
+        s_win = keep.tile([P, T], U8, name="s_win", tag="slot_s", align_bytes=64)
         nc.gpsimd.memset(s_win[:].bitcast(I32), 0)
         n_win = keep.tile([P, T], F32, name="n_win", align_bytes=64)
         nc.vector.memset(n_win[:], 0.0)
@@ -59,6 +58,7 @@ def tile_picked_ybocpd_post_p_kernel(tc, x_words, x_scales, hT, norm, post, haz,
         nc.gpsimd.dma_start(out=hs_rows[0:64, :], in_=haz[0:16, :].rearrange("r (b p) -> (r b) p", p=P))
         nc.gpsimd.dma_start(out=hs_rows[64:128, :], in_=start[0:16, :].rearrange("r (b p) -> (r b) p", p=P))
         load_h(0, 0, keep.tile([P, 4 * W], F32, name="h_raw00", tag="slot_b", align_bytes=64)[:])
+        nc.sync.dma_start(offsets[:], offs)
         for q in range(4):
             nc.sync.dma_start(out=s_win[32 * q:32 * q + 8, :].bitcast(I32),
                               in_=x_scales[:, 4 * q:4 * q + 4, :].bitcast(I32))
@@ -77,7 +77,7 @@ def tile_picked_ybocpd_post_p_kernel(tc, x_words, x_scales, hT, norm, post, haz,
         h_bf, h_codes, h_scales = {}, {}, {}
 
         def cast_h(c, g, eng):
-            h_bf[c, g] = keep.tile([P, W, 4], BF16, name="h_bf%d%d" % (c, g), tag="h_bf%d%d" % (c, g), align_bytes=64)
+            h_bf[c, g] = keep.tile([P, W, 4], BF16, name="h_bf%d%d" % (c, g), tag=("slot_a" if (c, g) == (1, 0) else "h_bf%d%d" % (c, g)), align_bytes=64)
             dst = h_bf[c, g][:].rearrange("p (c i) t -> p c t i", i=4)
             srcv = h_raw[c, g].rearrange("p t (c i) -> p c t i", i=4)
             if eng == "s":
@@ -93,8 +93,8 @@ def tile_picked_ybocpd_post_p_kernel(tc, x_words, x_scales, hT, norm, post, haz,
 
         cast_h(0, 0, "s")
         load_h(1, 0, keep.tile([P, 4 * W], F32, name="h_raw10", tag="slot_b", align_bytes=64)[:])
-        cast_h(0, 1, "s")
-        load_post(0, keep.tile([P, S], F32, name="post0", tag="slot_c", align_bytes=64)[:])
+        cast_h(0, 1, "v")
+        load_h(1, 1, keep.tile([P, 4 * W], F32, name="h_raw11", tag="slot_c", align_bytes=64)[:])
 
         n_pick = keep.tile([P, S], F32, name="n_pick")
         nc.vector.tensor_scalar(n_pick[:], n_win[:].indirect(offsets[:]), -0.7, 0.0, ALU.mult, ALU.add)
@@ -117,15 +117,20 @@ def tile_picked_ybocpd_post_p_kernel(tc, x_words, x_scales, hT, norm, post, haz,
         nc.scalar.activation(out=stay[:], in_=haz_ps[:], func=ACT.Copy, scale=-1.0, bias=1.0)
 
         quant_h(0, 0)
+        quant_h(0, 1)
+        late = keep.tile([P, NB * S], F32, name="late", tag="h_bf01", align_bytes=64)
+        for b in range(NB):
+            load_post(b, late[:, b * S:(b + 1) * S])
         s_pick = keep.tile([P, S], U8, name="s_pick", align_bytes=64)
         nc.vector.tensor_copy(s_pick[:], s_win[:].indirect(offsets[:]))
-        quant_h(0, 1)
-        late = keep.tile([P, 4 * W + 3 * S], F32, name="late", tag="h_bf01", align_bytes=64)
-        load_h(1, 1, late[:, 0:4 * W])
-        for b in range(1, NB):
-            load_post(b, late[:, 4 * W + (b - 1) * S:4 * W + b * S])
-        x_pick = [keep.tile([P, S], U32, name="x_pick%d" % g, align_bytes=64) for g in range(PASSES)]
-        nc.vector.tensor_copy(x_pick[0][:], x_win[0].bitcast(U32).indirect(offsets[:]))
+        x_both = keep.tile([P, PASSES * S], U32, name="x_both", tag="slot_s", align_bytes=64)
+        x_pick = [x_both[:, g * S:(g + 1) * S] for g in range(PASSES)]
+        nc.vector.tensor_copy(x_pick[0], x_win[0].bitcast(U32).indirect(offsets[:]))
+        spin = psum.tile([P, 2 * W], F32, name="spin", tag="e", bufs=2)
+        for u in range(4):
+            nc.tensor.matmul_mx(out=spin[:, (u % 2) * W:(u % 2 + 1) * W], lhsT=h_codes[0, 0][:, 0:P].bitcast(FP8X4),
+                                lhsT_scale=s_pick[:, 0:P], rhs=h_codes[0, 0][:].bitcast(FP8X4),
+                                rhs_scale=h_scales[0, 0][:], start=True, stop=True)
 
         sums = {}
 
@@ -139,8 +144,8 @@ def tile_picked_ybocpd_post_p_kernel(tc, x_words, x_scales, hT, norm, post, haz,
 
         dens = keep.tile([P, NB, V], F32, name="dens")
 
-        def exp_of(c, jb):
-            nc.scalar.activation(out=dens[:, jb, c * W:(c + 1) * W], in_=sums[c, jb][:], func=ACT.Exp,
+        def exp_of(c, jb, lo, hi):
+            nc.scalar.activation(out=dens[:, jb, c * W + lo:c * W + hi], in_=sums[c, jb][:, lo:hi], func=ACT.Exp,
                                  bias=bias[:, jb:jb + 1], scale=0.7)
 
         for jb in range(NB):
@@ -150,7 +155,7 @@ def tile_picked_ybocpd_post_p_kernel(tc, x_words, x_scales, hT, norm, post, haz,
                                   x_win[1].bitcast(U32).indirect(offsets[:, half * 16:(half + 1) * 16]))
             for jb in (2 * half, 2 * half + 1):
                 mx_pass(0, 1, jb)
-                exp_of(0, jb)
+                exp_of(0, jb, 0, P if half else W)
 
         joint = {}
         stats = {}
@@ -178,29 +183,31 @@ def tile_picked_ybocpd_post_p_kernel(tc, x_words, x_scales, hT, norm, post, haz,
             if eng == "s":
                 nc.scalar.activation(out=stats[b][:, 3:4], in_=stats[b][:, 2:3], func=ACT.Copy, scale=100.0)
                 nc.scalar.activation(out=res[:], in_=nw[:], func=ACT.Copy, scale=stats[b][:, 3:4])
-            elif eng == "g":
-                nc.gpsimd.tensor_scalar(res[:], nw[:], stats[b][:, 2:3], 100.0, ALU.mult, ALU.mult)
+                nc.sync.dma_start(out=out[b * P:(b + 1) * P, :], in_=res[:])
             else:
-                nc.vector.tensor_scalar(res[:], nw[:], stats[b][:, 2:3], 100.0, ALU.mult, ALU.mult)
-            nc.sync.dma_start(out=out[b * P:(b + 1) * P, :], in_=res[:])
+                for cols, queue in ((slice(0, S // 2), nc.sync), (slice(S // 2, S), nc.scalar)):
+                    nc.vector.tensor_scalar(res[:, cols], nw[:, cols], stats[b][:, 2:3], 100.0, ALU.mult, ALU.mult)
+                    queue.dma_start(out=out[b * P:(b + 1) * P, cols], in_=res[:, cols])
 
-        cast_h(1, 0, "v")
-        quant_h(1, 0)
+        for g in range(PASSES):
+            cast_h(1, g, "v")
+            quant_h(1, g)
         turn(0)
-        cast_h(1, 1, "s")
+        for jb in (2, 3):
+            exp_of(0, jb, P, W)
         change(0)
         turn(1)
-        quant_h(1, 1)
+        for g in range(PASSES):
+            for jb in range(NB):
+                mx_pass(1, g, jb)
         for jb in range(NB):
-            mx_pass(1, 0, jb)
-            mx_pass(1, 1, jb)
-            exp_of(1, jb)
+            exp_of(1, jb, 0, W)
+        turn(2)
         finish(0, "s")
+        turn(3)
         change(1)
         finish(1, "s")
-        turn(2)
         change(2)
-        turn(3)
         finish(2, "s")
         change(3)
         finish(3, "v")

@@ -54,9 +54,6 @@ def tile_picked_ybocpd_post_p_kernel(tc, x_words, x_scales, hT, norm, post, haz,
         nc.gpsimd.memset(s_win[:].bitcast(I32), 0)
         n_win = keep.tile([P, T], F32, name="n_win", align_bytes=64)
         nc.vector.memset(n_win[:], 0.0)
-        hs_rows = keep.tile([P, P], F32, name="hs_rows")
-        nc.gpsimd.dma_start(out=hs_rows[0:64, :], in_=haz[0:16, :].rearrange("r (b p) -> (r b) p", p=P))
-        nc.gpsimd.dma_start(out=hs_rows[64:128, :], in_=start[0:16, :].rearrange("r (b p) -> (r b) p", p=P))
         load_h(0, 0, keep.tile([P, 4 * W], F32, name="h_raw00", tag="slot_b", align_bytes=64)[:])
         nc.sync.dma_start(offsets[:], offs)
         for q in range(4):
@@ -92,7 +89,11 @@ def tile_picked_ybocpd_post_p_kernel(tc, x_words, x_scales, hT, norm, post, haz,
                                   in_=h_bf[c, g][:].rearrange("p w j -> p (w j)"))
 
         cast_h(0, 0, "s")
-        load_h(1, 0, keep.tile([P, 4 * W], F32, name="h_raw10", tag="slot_b", align_bytes=64)[:])
+        mid = keep.tile([P, 4 * W + P], F32, name="mid", tag="slot_b", align_bytes=64)
+        hs_rows = mid[:, 4 * W:4 * W + P]
+        nc.sync.dma_start(out=hs_rows[0:64, :], in_=haz[0:16, :].rearrange("r (b p) -> (r b) p", p=P))
+        nc.sync.dma_start(out=hs_rows[64:128, :], in_=start[0:16, :].rearrange("r (b p) -> (r b) p", p=P))
+        load_h(1, 0, mid[:, 0:4 * W])
         cast_h(0, 1, "v")
         load_h(1, 1, keep.tile([P, 4 * W], F32, name="h_raw11", tag="slot_c", align_bytes=64)[:])
 
@@ -102,19 +103,7 @@ def tile_picked_ybocpd_post_p_kernel(tc, x_words, x_scales, hT, norm, post, haz,
         for jb in range(NB):
             nc.tensor.transpose(n_ps[:, jb, :], n_pick[:, jb * P:(jb + 1) * P], ident[:])
         bias = keep.tile([P, NB], F32, name="bias")
-        nc.vector.tensor_copy(out=bias[:], in_=n_ps[:, :, NROW])
-
-        hs_ps = psum.tile([P, P], F32, name="hs_ps", tag="e", bufs=2)
-        nc.tensor.transpose(hs_ps[:], hs_rows[:], ident[:])
-        hs_cols = keep.tile([P, 2, NB], F32, name="hs_cols")
-        nc.vector.tensor_copy(out=hs_cols[:], in_=hs_ps[:].rearrange("p (a r) -> p a r", a=2)[:, :, 0:NB])
-        haz_ps = psum.tile([P, S], F32, name="haz_ps")
-        start_ps = psum.tile([P, S], F32, name="start_ps")
-        for a, bank in enumerate((haz_ps, start_ps)):
-            for jb in range(NB):
-                nc.tensor.transpose(bank[:, jb * P:(jb + 1) * P], hs_cols[:, a, jb:jb + 1].to_broadcast([P, P]), ident[:])
-        stay = keep.tile([P, S], F32, name="stay")
-        nc.scalar.activation(out=stay[:], in_=haz_ps[:], func=ACT.Copy, scale=-1.0, bias=1.0)
+        nc.scalar.copy(out=bias[:], in_=n_ps[:, :, NROW])
 
         quant_h(0, 0)
         quant_h(0, 1)
@@ -157,6 +146,18 @@ def tile_picked_ybocpd_post_p_kernel(tc, x_words, x_scales, hT, norm, post, haz,
                 mx_pass(0, 1, jb)
                 exp_of(0, jb, 0, P if half else W)
 
+        hs_ps = psum.tile([P, P], F32, name="hs_ps", tag="e", bufs=2)
+        nc.tensor.transpose(hs_ps[:], hs_rows, ident[:])
+        hs_cols = keep.tile([P, 2, NB], F32, name="hs_cols")
+        nc.scalar.copy(out=hs_cols[:], in_=hs_ps[:].rearrange("p (a r) -> p a r", a=2)[:, :, 0:NB])
+        haz_ps = psum.tile([P, S], F32, name="haz_ps")
+        start_ps = psum.tile([P, S], F32, name="start_ps")
+        for a, bank in enumerate((haz_ps, start_ps)):
+            for jb in range(NB):
+                nc.tensor.transpose(bank[:, jb * P:(jb + 1) * P], hs_cols[:, a, jb:jb + 1].to_broadcast([P, P]), ident[:])
+        stay = keep.tile([P, S], F32, name="stay")
+        nc.scalar.activation(out=stay[:], in_=haz_ps[:], func=ACT.Copy, scale=-1.0, bias=1.0)
+
         joint = {}
         stats = {}
 
@@ -174,15 +175,21 @@ def tile_picked_ybocpd_post_p_kernel(tc, x_words, x_scales, hT, norm, post, haz,
             nc.vector.scalar_tensor_tensor(out=ch[:], in0=haz_ps[:], scalar=1.0, in1=joint[b][:],
                                            op0=ALU.mult, op1=ALU.mult, accum_out=stats[b][:, 0:1])
 
-        def finish(b, eng):
-            nw = keep.tile([P, S], F32, name="nw%d" % b)
-            nc.vector.scalar_tensor_tensor(out=nw[:], in0=start_ps[:], scalar=stats[b][:, 0:1], in1=grown[:, b, :],
-                                           op0=ALU.mult, op1=ALU.add, accum_out=stats[b][:, 1:2])
-            nc.vector.reciprocal(out=stats[b][:, 2:3], in_=stats[b][:, 1:2])
+        weights = {}
+
+        def finish(b):
+            nw = post_sb[(b + 2) % NB] if b % 2 else keep.tile([P, S], F32, name="nw%d" % b)[:]
+            nc.vector.scalar_tensor_tensor(out=nw, in0=start_ps[:], scalar=stats[b][:, 0:1], in1=grown[:, b, :],
+                                           op0=ALU.mult, op1=ALU.add, accum_out=stats[min(b, 2)][:, 1:2])
+            weights[b] = nw
+
+        def normalise(b, eng):
+            nw = weights[b]
+            nc.vector.reciprocal(out=stats[b][:, 2:3], in_=stats[min(b, 2)][:, 1:2])
             res = keep.tile([P, S], F32, name="res%d" % b)
             if eng == "s":
                 nc.scalar.activation(out=stats[b][:, 3:4], in_=stats[b][:, 2:3], func=ACT.Copy, scale=100.0)
-                nc.scalar.activation(out=res[:], in_=nw[:], func=ACT.Copy, scale=stats[b][:, 3:4])
+                nc.scalar.activation(out=res[:], in_=nw, func=ACT.Copy, scale=stats[b][:, 3:4])
                 nc.sync.dma_start(out=out[b * P:(b + 1) * P, :], in_=res[:])
             else:
                 for cols, queue in ((slice(0, S // 2), nc.sync), (slice(S // 2, S), nc.scalar)):
@@ -195,7 +202,6 @@ def tile_picked_ybocpd_post_p_kernel(tc, x_words, x_scales, hT, norm, post, haz,
         turn(0)
         for jb in (2, 3):
             exp_of(0, jb, P, W)
-        change(0)
         turn(1)
         for g in range(PASSES):
             for jb in range(NB):
@@ -203,11 +209,16 @@ def tile_picked_ybocpd_post_p_kernel(tc, x_words, x_scales, hT, norm, post, haz,
         for jb in range(NB):
             exp_of(1, jb, 0, W)
         turn(2)
-        finish(0, "s")
         turn(3)
+        change(0)
         change(1)
-        finish(1, "s")
+        finish(0)
+        normalise(0, "s")
+        finish(1)
         change(2)
-        finish(2, "s")
+        normalise(1, "s")
         change(3)
-        finish(3, "v")
+        finish(2)
+        normalise(2, "s")
+        finish(3)
+        normalise(3, "v")

@@ -20,67 +20,88 @@ ALU = mybir.AluOpType
 ACT = mybir.ActivationFunctionType
 
 W = 256
-NROW = 16
+PARK = 96
+NORM_ROW = P - 1
+HS_ROW = P - 2 * NB
+RAW_BYTES = 4 * W * 4
+ROW_BYTES = S * 4
+HALF_ROW = ROW_BYTES // 2
+NORM_AT = 2 * RAW_BYTES + HALF_ROW
+CAST_AT = NORM_AT + T * 4 + HALF_ROW
 
 
 def tile_picked_ybocpd_post_p_kernel(tc, x_words, x_scales, hT, norm, post, haz, start, offs, out):
     nc = tc.nc
     with ExitStack() as ctx:
         keep = ctx.enter_context(tc.tile_pool(name="keep", bufs=1))
+        over = ctx.enter_context(tc.tile_pool(name="over", bufs=1))
         psum = ctx.enter_context(tc.psum_pool(name="psum", bufs=1))
 
-        offsets = keep.tile([P, S // 16], U16, name="offsets")
+        def h_rows(c, g):
+            return hT[512 * g:512 * (g + 1), c * W:(c + 1) * W].rearrange("(p j) w -> p j w", j=4)
 
         h_raw = {}
-        post_sb = {}
+
+        def load_first_h(g):
+            h_raw[0, g] = keep.tile([P, 4, W], F32, name="h_raw0%d" % g)
+            nc.sync.dma_start(out=h_raw[0, g][:], in_=h_rows(0, g))
+
+        load_first_h(0)
+        offsets = keep.tile([P, S // 16], U16, name="offsets")
+        nc.sync.dma_start(offsets[:], offs)
+        s_win = over.tile([P, T], U8, name="s_win", offset=RAW_BYTES - T // 2)
+        nc.sync.dma_start(out=s_win[PARK:P, :].bitcast(I32),
+                            in_=x_scales.bitcast(I32).rearrange("g m n -> m g n"))
+        n_win = over.tile([P, T], F32, name="n_win", offset=NORM_AT)
+        nc.sync.dma_start(out=n_win[NORM_ROW:P, :], in_=norm[0:1, :])
+        hs_rows = keep.tile([P, P], F32, name="hs_rows")
+        nc.sync.dma_start(out=hs_rows[HS_ROW:HS_ROW + NB, :], in_=haz[0:1, :].rearrange("r (b p) -> (r b) p", p=P))
+        nc.sync.dma_start(out=hs_rows[HS_ROW + NB:P, :], in_=start[0:1, :].rearrange("r (b p) -> (r b) p", p=P))
+
+        load_first_h(1)
         x_win = {}
-
-        def load_h(c, g, dst):
-            h_raw[c, g] = dst.rearrange("p (j w) -> p j w", j=4)
-            nc.sync.dma_start(out=h_raw[c, g],
-                              in_=hT[512 * g:512 * (g + 1), c * W:(c + 1) * W].rearrange("(p j) w -> p j w", j=4))
-
-        def load_post(b, dst):
-            post_sb[b] = dst
-            nc.sync.dma_start(out=dst, in_=post[b * P:(b + 1) * P, :])
-
-        def load_x(g, dst):
-            x_win[g] = dst
-            nc.sync.dma_start(out=dst, in_=x_words[g].rearrange("p n t -> p (n t)").bitcast(I32))
+        for g in range(PASSES):
+            x_win[g] = keep.tile([P, T], I32, name="x_win%d" % g, align_bytes=64)
+            nc.sync.dma_start(out=x_win[g][:], in_=x_words[g].rearrange("p n t -> p (n t)").bitcast(I32))
 
         grown = keep.tile([P, NB, S], F32, name="grown")
         nc.gpsimd.memset(grown[:, :, 0:1], 0.0)
-        s_win = keep.tile([P, T], U8, name="s_win", tag="slot_s", align_bytes=64)
-        nc.gpsimd.memset(s_win[:].bitcast(I32), 0)
-        n_win = keep.tile([P, T], F32, name="n_win", align_bytes=64)
-        nc.vector.memset(n_win[:], 0.0)
-        load_h(0, 0, keep.tile([P, 4 * W], F32, name="h_raw00", tag="slot_b", align_bytes=64)[:])
-        nc.sync.dma_start(offsets[:], offs)
-        for q in range(4):
-            nc.sync.dma_start(out=s_win[32 * q:32 * q + 8, :].bitcast(I32),
-                              in_=x_scales[:, 4 * q:4 * q + 4, :].bitcast(I32))
-        nc.sync.dma_start(out=n_win[NROW:NROW + 1, :], in_=norm[0:1, :])
-        load_h(0, 1, keep.tile([P, 4 * W], F32, name="h_raw01", tag="slot_c", align_bytes=64)[:])
-
+        one = keep.tile([P, 1], F32, name="one")
+        nc.scalar.activation(out=one[:], in_=grown[:, 0, 0:1], func=ACT.Exp)
+        nc.vector.memset(s_win[0:PARK, :].bitcast(I32), 0)
+        nc.vector.memset(n_win[0:NORM_ROW, :], 0.0)
+        s_plane = keep.tile([P, PASSES * S], U8, name="s_plane", align_bytes=64)
+        nc.gpsimd.memset(s_plane[:].bitcast(I32), 0)
+        nc.gpsimd.memset(hs_rows[0:HS_ROW, :], 0.0)
         ident = keep.tile([P, P], F32, name="ident")
         make_identity(nc, ident[:])
 
-        warm = keep.tile([P, 1], F32, name="warm", tag="slot_a", align_bytes=64)
-        nc.scalar.activation(out=warm[:], in_=grown[:, 0, 0:1], func=ACT.Exp)
-        x_all = keep.tile([P, PASSES * T], I32, name="x_all", tag="slot_a", align_bytes=64)
-        load_x(0, x_all[:, 0:T])
-        load_x(1, x_all[:, T:2 * T])
+        s_pick = keep.tile([P, S], U8, name="s_pick", align_bytes=64)
+        nc.vector.tensor_copy(s_pick[:], s_win[:].indirect(offsets[:]))
+        for q in range(4):
+            nc.sync.dma_start(out=s_plane[32 * q:32 * q + 4, :].bitcast(I32).rearrange("r (g n) -> r g n", g=PASSES),
+                                in_=s_pick[PARK + 8 * q:PARK + 8 * q + 8, :].bitcast(I32))
+        for g in range(PASSES):
+            h_raw[1, g] = over.tile([P, 4, W], F32, name="h_raw1%d" % g, offset=g * RAW_BYTES)
+            nc.sync.dma_start(out=h_raw[1, g][:], in_=h_rows(1, g))
+
+        n_pick = keep.tile([P, S], F32, name="n_pick")
+        nc.vector.tensor_scalar(n_pick[:], n_win[:].indirect(offsets[:]), -0.7, 0.0, ALU.mult, ALU.add)
+        post_sb = {}
+        for b in range(NB):
+            post_sb[b] = over.tile([P, S], F32, name="post%d" % b, offset=NORM_AT + HALF_ROW + b * ROW_BYTES)
+            nc.sync.dma_start(out=post_sb[b][:], in_=post[b * P:(b + 1) * P, :])
 
         h_bf, h_codes, h_scales = {}, {}, {}
 
-        def cast_h(c, g, eng):
-            h_bf[c, g] = keep.tile([P, W, 4], BF16, name="h_bf%d%d" % (c, g), tag=("slot_a" if (c, g) == (1, 0) else "h_bf%d%d" % (c, g)), align_bytes=64)
-            dst = h_bf[c, g][:].rearrange("p (c i) t -> p c t i", i=4)
-            srcv = h_raw[c, g].rearrange("p t (c i) -> p c t i", i=4)
-            if eng == "s":
-                nc.scalar.copy(out=dst, in_=srcv)
+        def cast_h(c, g, copy):
+            if (c, g) == (1, 1):
+                h_bf[c, g] = keep.tile([P, W, 4], BF16, name="h_bf11", tag="dens0", align_bytes=64)
             else:
-                nc.vector.tensor_copy(out=dst, in_=srcv)
+                h_bf[c, g] = over.tile([P, W, 4], BF16, name="h_bf%d%d" % (c, g), align_bytes=64,
+                                       offset=CAST_AT + (3 * HALF_ROW if c else g * ROW_BYTES))
+            copy(out=h_bf[c, g][:].rearrange("p (c i) t -> p c t i", i=4),
+                 in_=h_raw[c, g][:].rearrange("p t (c i) -> p c t i", i=4))
 
         def quant_h(c, g):
             h_codes[c, g] = keep.tile([P, W], U32, name="h_codes%d%d" % (c, g), align_bytes=64)
@@ -88,85 +109,63 @@ def tile_picked_ybocpd_post_p_kernel(tc, x_words, x_scales, hT, norm, post, haz,
             nc.vector.quantize_mx(out=h_codes[c, g][:].bitcast(FP8X4), scales=h_scales[c, g][:],
                                   in_=h_bf[c, g][:].rearrange("p w j -> p (w j)"))
 
-        cast_h(0, 0, "s")
-        mid = keep.tile([P, 4 * W + P], F32, name="mid", tag="slot_b", align_bytes=64)
-        hs_rows = mid[:, 4 * W:4 * W + P]
-        nc.sync.dma_start(out=hs_rows[0:64, :], in_=haz[0:16, :].rearrange("r (b p) -> (r b) p", p=P))
-        nc.sync.dma_start(out=hs_rows[64:128, :], in_=start[0:16, :].rearrange("r (b p) -> (r b) p", p=P))
-        load_h(1, 0, mid[:, 0:4 * W])
-        cast_h(0, 1, "v")
-        load_h(1, 1, keep.tile([P, 4 * W], F32, name="h_raw11", tag="slot_c", align_bytes=64)[:])
+        for g in range(PASSES):
+            cast_h(0, g, nc.scalar.copy)
+            quant_h(0, g)
 
-        n_pick = keep.tile([P, S], F32, name="n_pick")
-        nc.vector.tensor_scalar(n_pick[:], n_win[:].indirect(offsets[:]), -0.7, 0.0, ALU.mult, ALU.add)
-        n_ps = psum.tile([P, NB, P], F32, name="n_ps", tag="e", bufs=2)
-        for jb in range(NB):
-            nc.tensor.transpose(n_ps[:, jb, :], n_pick[:, jb * P:(jb + 1) * P], ident[:])
-        bias = keep.tile([P, NB], F32, name="bias")
-        nc.scalar.copy(out=bias[:], in_=n_ps[:, :, NROW])
-
-        quant_h(0, 0)
-        quant_h(0, 1)
-        late = keep.tile([P, NB * S], F32, name="late", tag="h_bf01", align_bytes=64)
-        for b in range(NB):
-            load_post(b, late[:, b * S:(b + 1) * S])
-        s_pick = keep.tile([P, S], U8, name="s_pick", align_bytes=64)
-        nc.vector.tensor_copy(s_pick[:], s_win[:].indirect(offsets[:]))
-        x_both = keep.tile([P, PASSES * S], U32, name="x_both", tag="slot_s", align_bytes=64)
-        x_pick = [x_both[:, g * S:(g + 1) * S] for g in range(PASSES)]
-        nc.vector.tensor_copy(x_pick[0], x_win[0].bitcast(U32).indirect(offsets[:]))
-        spin = psum.tile([P, 2 * W], F32, name="spin", tag="e", bufs=2)
-        for u in range(4):
-            nc.tensor.matmul_mx(out=spin[:, (u % 2) * W:(u % 2 + 1) * W], lhsT=h_codes[0, 0][:, 0:P].bitcast(FP8X4),
-                                lhsT_scale=s_pick[:, 0:P], rhs=h_codes[0, 0][:].bitcast(FP8X4),
-                                rhs_scale=h_scales[0, 0][:], start=True, stop=True)
-
-        sums = {}
-
-        def mx_pass(c, g, jb):
-            if g == 0:
-                sums[c, jb] = psum.tile([P, W], F32, name="sums%d%d" % (c, jb), tag="sums%d" % jb)
-            cols = slice(jb * P, (jb + 1) * P)
-            nc.tensor.matmul_mx(out=sums[c, jb][:], lhsT=x_pick[g][:, cols].bitcast(FP8X4),
-                                lhsT_scale=s_pick[4 * g:P, cols], rhs=h_codes[c, g][:].bitcast(FP8X4),
-                                rhs_scale=h_scales[c, g][:], start=(g == 0), stop=(g == PASSES - 1))
-
-        dens = keep.tile([P, NB, V], F32, name="dens")
-
-        def exp_of(c, jb, lo, hi):
-            nc.scalar.activation(out=dens[:, jb, c * W + lo:c * W + hi], in_=sums[c, jb][:, lo:hi], func=ACT.Exp,
-                                 bias=bias[:, jb:jb + 1], scale=0.7)
-
-        for jb in range(NB):
-            mx_pass(0, 0, jb)
-        for half in range(2):
-            nc.vector.tensor_copy(x_pick[1][:, half * 256:(half + 1) * 256],
-                                  x_win[1].bitcast(U32).indirect(offsets[:, half * 16:(half + 1) * 16]))
-            for jb in (2 * half, 2 * half + 1):
-                mx_pass(0, 1, jb)
-                exp_of(0, jb, 0, P if half else W)
-
-        hs_ps = psum.tile([P, P], F32, name="hs_ps", tag="e", bufs=2)
-        nc.tensor.transpose(hs_ps[:], hs_rows, ident[:])
-        hs_cols = keep.tile([P, 2, NB], F32, name="hs_cols")
-        nc.scalar.copy(out=hs_cols[:], in_=hs_ps[:].rearrange("p (a r) -> p a r", a=2)[:, :, 0:NB])
+        hs_ps = psum.tile([P, P], F32, name="hs_ps", tag="turn", bufs=2)
+        nc.tensor.transpose(hs_ps[:], hs_rows[:], ident[:])
+        hs_cols = keep.tile([P, 2 * NB], F32, name="hs_cols")
+        nc.scalar.copy(out=hs_cols[:], in_=hs_ps[:, HS_ROW:P])
         haz_ps = psum.tile([P, S], F32, name="haz_ps")
         start_ps = psum.tile([P, S], F32, name="start_ps")
         for a, bank in enumerate((haz_ps, start_ps)):
             for jb in range(NB):
-                nc.tensor.transpose(bank[:, jb * P:(jb + 1) * P], hs_cols[:, a, jb:jb + 1].to_broadcast([P, P]), ident[:])
+                col = a * NB + jb
+                nc.tensor.transpose(bank[:, jb * P:(jb + 1) * P], hs_cols[:, col:col + 1].to_broadcast([P, P]), ident[:])
+        n_ps = psum.tile([P, NB, P], F32, name="n_ps", tag="turn", bufs=2)
+        for jb in range(NB):
+            nc.tensor.transpose(n_ps[:, jb, :], n_pick[:, jb * P:(jb + 1) * P], ident[:])
+        bias = keep.tile([P, NB], F32, name="bias")
+        nc.scalar.copy(out=bias[:], in_=n_ps[:, :, NORM_ROW])
         stay = keep.tile([P, S], F32, name="stay")
-        nc.scalar.activation(out=stay[:], in_=haz_ps[:], func=ACT.Copy, scale=-1.0, bias=1.0)
+        nc.scalar.activation(out=stay[:], in_=haz_ps[:], func=ACT.Identity, scale=-1.0, bias=one[:])
 
-        joint = {}
-        stats = {}
+        x_pick = {}
+        x_pick[0] = over.tile([P, S], U32, name="x_pick0", align_bytes=64, offset=NORM_AT - HALF_ROW)
+        nc.vector.tensor_copy(x_pick[0][:], x_win[0][:].bitcast(U32).indirect(offsets[:]))
+
+        sums = {}
+
+        def mx_half(b, g, half):
+            c, cols = b // 2, slice((b % 2) * P, (b % 2 + 1) * P)
+            if g == 0:
+                sums[b, half] = psum.tile([P, 2, P], F32, name="sums%d%d" % (b, half), tag="sums", bufs=4)
+            for u in range(2):
+                runs = slice((2 * half + u) * P, (2 * half + u + 1) * P)
+                nc.tensor.matmul_mx(out=sums[b, half][:, u, :], lhsT=x_pick[g][:, runs].bitcast(FP8X4),
+                                    lhsT_scale=s_plane[:, g * S + runs.start:g * S + runs.stop], rhs=h_codes[c, g][:, cols].bitcast(FP8X4),
+                                    rhs_scale=h_scales[c, g][:, cols],
+                                    start=(g == 0 and u == 0), stop=(g == PASSES - 1 and u == 1))
+
+        dens = {}
+
+        def exp_half(b, half):
+            if half == 0:
+                dens[b] = keep.tile([P, NB, P], F32, name="dens%d" % b, align_bytes=64)
+            for u in range(2):
+                jb = 2 * half + u
+                nc.scalar.activation(out=dens[b][:, jb, :], in_=sums[b, half][:, u, :], func=ACT.Exp,
+                                     bias=bias[:, jb:jb + 1], scale=0.7)
+
+        joint, stats, weights = {}, {}, {}
 
         def turn(b):
-            e_ps = psum.tile([P, S], F32, name="e_ps%d" % b, tag="e", bufs=2)
+            e_ps = psum.tile([P, S], F32, name="e_ps%d" % b, tag="turn", bufs=2)
             for jb in range(NB):
-                nc.tensor.transpose(e_ps[:, jb * P:(jb + 1) * P], dens[:, jb, b * P:(b + 1) * P], ident[:])
+                nc.tensor.transpose(e_ps[:, jb * P:(jb + 1) * P], dens[b][:, jb, :], ident[:])
             joint[b] = keep.tile([P, S], F32, name="joint%d" % b)
-            nc.vector.tensor_tensor(out=joint[b][:], in0=e_ps[:], in1=post_sb[b], op=ALU.mult)
+            nc.vector.tensor_tensor(out=joint[b][:], in0=e_ps[:], in1=post_sb[b][:], op=ALU.mult)
             nc.gpsimd.tensor_tensor(out=grown[:, b, 1:S], in0=joint[b][:, 0:S - 1], in1=stay[:, 0:S - 1], op=ALU.mult)
 
         def change(b):
@@ -175,50 +174,69 @@ def tile_picked_ybocpd_post_p_kernel(tc, x_words, x_scales, hT, norm, post, haz,
             nc.vector.scalar_tensor_tensor(out=ch[:], in0=haz_ps[:], scalar=1.0, in1=joint[b][:],
                                            op0=ALU.mult, op1=ALU.mult, accum_out=stats[b][:, 0:1])
 
-        weights = {}
-
         def finish(b):
-            nw = post_sb[(b + 2) % NB] if b % 2 else keep.tile([P, S], F32, name="nw%d" % b)[:]
-            nc.vector.scalar_tensor_tensor(out=nw, in0=start_ps[:], scalar=stats[b][:, 0:1], in1=grown[:, b, :],
-                                           op0=ALU.mult, op1=ALU.add, accum_out=stats[min(b, 2)][:, 1:2])
-            weights[b] = nw
+            weights[b] = keep.tile([P, S], F32, name="nw%d" % b)
+            nc.vector.scalar_tensor_tensor(out=weights[b][:], in0=start_ps[:], scalar=stats[b][:, 0:1], in1=grown[:, b, :],
+                                           op0=ALU.mult, op1=ALU.add, accum_out=stats[b][:, 1:2])
 
-        def normalise(b, eng):
-            nw = weights[b]
-            nc.vector.reciprocal(out=stats[b][:, 2:3], in_=stats[min(b, 2)][:, 1:2])
+        def invert(b):
+            nc.vector.reciprocal(out=stats[b][:, 2:3], in_=stats[b][:, 1:2])
+
+        def normalise_scalar(b):
             res = keep.tile([P, S], F32, name="res%d" % b)
-            if eng == "s":
-                nc.scalar.activation(out=stats[b][:, 3:4], in_=stats[b][:, 2:3], func=ACT.Copy, scale=100.0)
-                nc.scalar.activation(out=res[:], in_=nw, func=ACT.Copy, scale=stats[b][:, 3:4])
-                nc.sync.dma_start(out=out[b * P:(b + 1) * P, :], in_=res[:])
-            else:
-                for cols, queue in ((slice(0, S // 2), nc.sync), (slice(S // 2, S), nc.scalar)):
-                    nc.vector.tensor_scalar(res[:, cols], nw[:, cols], stats[b][:, 2:3], 100.0, ALU.mult, ALU.mult)
-                    queue.dma_start(out=out[b * P:(b + 1) * P, cols], in_=res[:, cols])
+            factor = keep.tile([P, 1], F32, name="factor%d" % b)
+            nc.scalar.activation(out=factor[:], in_=stats[b][:, 2:3], func=ACT.Copy, scale=100.0)
+            nc.scalar.activation(out=res[:], in_=weights[b][:], func=ACT.Copy, scale=factor[:])
+            nc.sync.dma_start(out=out[b * P:(b + 1) * P, :], in_=res[:])
 
-        for g in range(PASSES):
-            cast_h(1, g, "v")
-            quant_h(1, g)
+        def normalise_vector(b):
+            res = keep.tile([P, S], F32, name="res%d" % b)
+            for cols, queue in ((slice(0, S // 2), nc.sync), (slice(S // 2, S), nc.scalar)):
+                nc.vector.tensor_scalar(res[:, cols], weights[b][:, cols], stats[b][:, 2:3], 100.0, ALU.mult, ALU.mult)
+                queue.dma_start(out=out[b * P:(b + 1) * P, cols], in_=res[:, cols])
+
+        for b in range(2):
+            for half in range(2):
+                mx_half(b, 0, half)
+        x_pick[1] = over.tile([P, S], U32, name="x_pick1", align_bytes=64, offset=CAST_AT + HALF_ROW)
+        for half in range(2):
+            nc.vector.tensor_copy(x_pick[1][:, half * 256:(half + 1) * 256],
+                                  x_win[1][:].bitcast(U32).indirect(offsets[:, half * 16:(half + 1) * 16]))
+            mx_half(0, 1, half)
+            exp_half(0, half)
+        cast_h(1, 0, nc.vector.tensor_copy)
+        quant_h(1, 0)
         turn(0)
-        for jb in (2, 3):
-            exp_of(0, jb, P, W)
-        turn(1)
-        for g in range(PASSES):
-            for jb in range(NB):
-                mx_pass(1, g, jb)
-        for jb in range(NB):
-            exp_of(1, jb, 0, W)
-        turn(2)
-        turn(3)
+        for half in range(2):
+            mx_half(1, 1, half)
+            exp_half(1, half)
         change(0)
+        turn(1)
+        cast_h(1, 1, nc.scalar.copy)
+        quant_h(1, 1)
+        for b in (2, 3):
+            for half in range(2):
+                mx_half(b, 0, half)
+        for half in range(2):
+            mx_half(2, 1, half)
+            exp_half(2, half)
         change(1)
         finish(0)
-        normalise(0, "s")
+        turn(2)
+        for half in range(2):
+            mx_half(3, 1, half)
+            exp_half(3, half)
+        invert(0)
+        normalise_scalar(0)
         finish(1)
         change(2)
-        normalise(1, "s")
-        change(3)
+        invert(1)
+        normalise_scalar(1)
+        turn(3)
         finish(2)
-        normalise(2, "s")
+        change(3)
+        invert(2)
+        normalise_scalar(2)
         finish(3)
-        normalise(3, "v")
+        invert(3)
+        normalise_vector(3)

@@ -26,8 +26,10 @@ HS_ROW = P - 2 * NB
 RAW_BYTES = 4 * W * 4
 ROW_BYTES = S * 4
 HALF_ROW = ROW_BYTES // 2
-NORM_AT = 2 * RAW_BYTES + HALF_ROW
-CAST_AT = NORM_AT + T * 4 + HALF_ROW
+WIN_BYTES = T * 4
+NORM_AT = WIN_BYTES + RAW_BYTES + HALF_ROW
+FIRST_AT = NORM_AT + WIN_BYTES
+CAST_AT = FIRST_AT + RAW_BYTES
 
 
 def tile_picked_ybocpd_post_p_kernel(tc, x_words, x_scales, hT, norm, post, haz, start, offs, out):
@@ -42,32 +44,46 @@ def tile_picked_ybocpd_post_p_kernel(tc, x_words, x_scales, hT, norm, post, haz,
 
         h_raw = {}
 
-        def load_first_h(g):
-            h_raw[0, g] = keep.tile([P, 4, W], F32, name="h_raw0%d" % g)
-            nc.sync.dma_start(out=h_raw[0, g][:], in_=h_rows(0, g))
+        def load_h(c, g, tile):
+            h_raw[c, g] = tile
+            nc.sync.dma_start(out=tile[:], in_=h_rows(c, g))
 
-        load_first_h(0)
+        x_win = {}
+
+        def load_x(g, tile):
+            x_win[g] = tile
+            nc.sync.dma_start(out=tile[:], in_=x_words[g].rearrange("p n t -> p (n t)").bitcast(I32))
+
+        post_sb = {}
+
+        def load_post(b, at):
+            post_sb[b] = over.tile([P, S], F32, name="post%d" % b, offset=at)
+            nc.sync.dma_start(out=post_sb[b][:], in_=post[b * P:(b + 1) * P, :])
+
         offsets = keep.tile([P, S // 16], U16, name="offsets")
         nc.sync.dma_start(offsets[:], offs)
-        s_win = over.tile([P, T], U8, name="s_win", offset=RAW_BYTES - T // 2)
+        s_win = over.tile([P, T], U8, name="s_win", offset=WIN_BYTES - T // 2)
         nc.sync.dma_start(out=s_win[PARK:P, :].bitcast(I32),
                             in_=x_scales.bitcast(I32).rearrange("g m n -> m g n"))
+        load_h(0, 0, keep.tile([P, 4, W], F32, name="h_raw00"))
         n_win = over.tile([P, T], F32, name="n_win", offset=NORM_AT)
         nc.sync.dma_start(out=n_win[NORM_ROW:P, :], in_=norm[0:1, :])
         hs_rows = keep.tile([P, P], F32, name="hs_rows")
         nc.sync.dma_start(out=hs_rows[HS_ROW:HS_ROW + NB, :], in_=haz[0:1, :].rearrange("r (b p) -> (r b) p", p=P))
         nc.sync.dma_start(out=hs_rows[HS_ROW + NB:P, :], in_=start[0:1, :].rearrange("r (b p) -> (r b) p", p=P))
 
-        load_first_h(1)
-        x_win = {}
-        for g in range(PASSES):
-            x_win[g] = keep.tile([P, T], I32, name="x_win%d" % g, align_bytes=64)
-            nc.sync.dma_start(out=x_win[g][:], in_=x_words[g].rearrange("p n t -> p (n t)").bitcast(I32))
+        load_h(0, 1, over.tile([P, 4, W], F32, name="h_raw01", offset=FIRST_AT))
+        load_x(0, keep.tile([P, T], I32, name="x_win0", align_bytes=64))
 
-        grown = keep.tile([P, NB, S], F32, name="grown")
-        nc.gpsimd.memset(grown[:, :, 0:1], 0.0)
+        joint = {}
+        for b in range(NB):
+            joint[b] = keep.tile([P, S + 1], F32, name="joint%d" % b)
+        stay = keep.tile([P, S + 1], F32, name="stay")
+        nc.gpsimd.memset(stay[:, 0:1], 0.0)
         one = keep.tile([P, 1], F32, name="one")
-        nc.scalar.activation(out=one[:], in_=grown[:, 0, 0:1], func=ACT.Exp)
+        nc.scalar.activation(out=one[:], in_=stay[:, 0:1], func=ACT.Exp)
+        for b in range(NB):
+            nc.gpsimd.memset(joint[b][:, 0:1], 0.0)
         nc.vector.memset(s_win[0:PARK, :].bitcast(I32), 0)
         nc.vector.memset(n_win[0:NORM_ROW, :], 0.0)
         s_plane = keep.tile([P, PASSES * S], U8, name="s_plane", align_bytes=64)
@@ -81,37 +97,39 @@ def tile_picked_ybocpd_post_p_kernel(tc, x_words, x_scales, hT, norm, post, haz,
         for q in range(4):
             nc.sync.dma_start(out=s_plane[32 * q:32 * q + 4, :].bitcast(I32).rearrange("r (g n) -> r g n", g=PASSES),
                                 in_=s_pick[PARK + 8 * q:PARK + 8 * q + 8, :].bitcast(I32))
-        for g in range(PASSES):
-            h_raw[1, g] = over.tile([P, 4, W], F32, name="h_raw1%d" % g, offset=g * RAW_BYTES)
-            nc.sync.dma_start(out=h_raw[1, g][:], in_=h_rows(1, g))
+        load_x(1, over.tile([P, T], I32, name="x_win1", offset=0))
+        load_h(1, 0, over.tile([P, 4, W], F32, name="h_raw10", offset=WIN_BYTES))
 
         n_pick = keep.tile([P, S], F32, name="n_pick")
         nc.vector.tensor_scalar(n_pick[:], n_win[:].indirect(offsets[:]), -0.7, 0.0, ALU.mult, ALU.add)
-        post_sb = {}
-        for b in range(NB):
-            post_sb[b] = over.tile([P, S], F32, name="post%d" % b, offset=NORM_AT + HALF_ROW + b * ROW_BYTES)
-            nc.sync.dma_start(out=post_sb[b][:], in_=post[b * P:(b + 1) * P, :])
+        load_h(1, 1, over.tile([P, 4, W], F32, name="h_raw11", offset=NORM_AT + HALF_ROW))
+        load_post(0, NORM_AT - HALF_ROW)
+        load_post(1, NORM_AT + HALF_ROW + RAW_BYTES)
 
         h_bf, h_codes, h_scales = {}, {}, {}
 
-        def cast_h(c, g, copy):
-            if (c, g) == (1, 1):
-                h_bf[c, g] = keep.tile([P, W, 4], BF16, name="h_bf11", tag="dens0", align_bytes=64)
-            else:
-                h_bf[c, g] = over.tile([P, W, 4], BF16, name="h_bf%d%d" % (c, g), align_bytes=64,
-                                       offset=CAST_AT + (3 * HALF_ROW if c else g * ROW_BYTES))
-            copy(out=h_bf[c, g][:].rearrange("p (c i) t -> p c t i", i=4),
-                 in_=h_raw[c, g][:].rearrange("p t (c i) -> p c t i", i=4))
+        def cast_h(blocks, g, copy, tile):
+            c, first = blocks[0] // 2, (blocks[0] % 2) * P
+            h_bf[blocks, g] = tile
+            copy(out=tile[:].rearrange("p (c i) t -> p c t i", i=4),
+                 in_=h_raw[c, g][:, :, first:first + P * len(blocks)].rearrange("p t (c i) -> p c t i", i=4))
 
-        def quant_h(c, g):
-            h_codes[c, g] = keep.tile([P, W], U32, name="h_codes%d%d" % (c, g), align_bytes=64)
-            h_scales[c, g] = keep.tile([P, W], U8, name="h_scales%d%d" % (c, g), align_bytes=64)
-            nc.vector.quantize_mx(out=h_codes[c, g][:].bitcast(FP8X4), scales=h_scales[c, g][:],
-                                  in_=h_bf[c, g][:].rearrange("p w j -> p (w j)"))
+        def quant_h(blocks, g):
+            width = P * len(blocks)
+            codes = keep.tile([P, width], U32, name="h_codes%d%d" % (blocks[0], g), align_bytes=64)
+            scales = keep.tile([P, width], U8, name="h_scales%d%d" % (blocks[0], g), align_bytes=64)
+            nc.vector.quantize_mx(out=codes[:].bitcast(FP8X4), scales=scales[:],
+                                  in_=h_bf[blocks, g][:].rearrange("p w j -> p (w j)"))
+            for i, b in enumerate(blocks):
+                h_codes[b, g] = codes[:, i * P:(i + 1) * P]
+                h_scales[b, g] = scales[:, i * P:(i + 1) * P]
 
         for g in range(PASSES):
-            cast_h(0, g, nc.scalar.copy)
-            quant_h(0, g)
+            cast_h((0, 1), g, nc.scalar.copy,
+                   over.tile([P, W, 4], BF16, name="h_bf0%d" % g, align_bytes=64, offset=CAST_AT + g * ROW_BYTES))
+            quant_h((0, 1), g)
+        load_post(2, FIRST_AT)
+        load_post(3, FIRST_AT + ROW_BYTES)
 
         hs_ps = psum.tile([P, P], F32, name="hs_ps", tag="turn", bufs=2)
         nc.tensor.transpose(hs_ps[:], hs_rows[:], ident[:])
@@ -128,24 +146,22 @@ def tile_picked_ybocpd_post_p_kernel(tc, x_words, x_scales, hT, norm, post, haz,
             nc.tensor.transpose(n_ps[:, jb, :], n_pick[:, jb * P:(jb + 1) * P], ident[:])
         bias = keep.tile([P, NB], F32, name="bias")
         nc.scalar.copy(out=bias[:], in_=n_ps[:, :, NORM_ROW])
-        stay = keep.tile([P, S], F32, name="stay")
-        nc.scalar.activation(out=stay[:], in_=haz_ps[:], func=ACT.Identity, scale=-1.0, bias=one[:])
+        nc.scalar.activation(out=stay[:, 1:S + 1], in_=haz_ps[:], func=ACT.Identity, scale=-1.0, bias=one[:])
 
         x_pick = {}
-        x_pick[0] = over.tile([P, S], U32, name="x_pick0", align_bytes=64, offset=NORM_AT - HALF_ROW)
+        x_pick[0] = keep.tile([P, S], U32, name="x_pick0", align_bytes=64)
         nc.vector.tensor_copy(x_pick[0][:], x_win[0][:].bitcast(U32).indirect(offsets[:]))
 
         sums = {}
 
         def mx_half(b, g, half):
-            c, cols = b // 2, slice((b % 2) * P, (b % 2 + 1) * P)
             if g == 0:
                 sums[b, half] = psum.tile([P, 2, P], F32, name="sums%d%d" % (b, half), tag="sums", bufs=4)
             for u in range(2):
                 runs = slice((2 * half + u) * P, (2 * half + u + 1) * P)
                 nc.tensor.matmul_mx(out=sums[b, half][:, u, :], lhsT=x_pick[g][:, runs].bitcast(FP8X4),
-                                    lhsT_scale=s_plane[:, g * S + runs.start:g * S + runs.stop], rhs=h_codes[c, g][:, cols].bitcast(FP8X4),
-                                    rhs_scale=h_scales[c, g][:, cols],
+                                    lhsT_scale=s_plane[:, g * S + runs.start:g * S + runs.stop], rhs=h_codes[b, g].bitcast(FP8X4),
+                                    rhs_scale=h_scales[b, g],
                                     start=(g == 0 and u == 0), stop=(g == PASSES - 1 and u == 1))
 
         dens = {}
@@ -158,25 +174,27 @@ def tile_picked_ybocpd_post_p_kernel(tc, x_words, x_scales, hT, norm, post, haz,
                 nc.scalar.activation(out=dens[b][:, jb, :], in_=sums[b, half][:, u, :], func=ACT.Exp,
                                      bias=bias[:, jb:jb + 1], scale=0.7)
 
-        joint, stats, weights = {}, {}, {}
+        grown, stats, weights = {}, {}, {}
 
         def turn(b):
             e_ps = psum.tile([P, S], F32, name="e_ps%d" % b, tag="turn", bufs=2)
             for jb in range(NB):
                 nc.tensor.transpose(e_ps[:, jb * P:(jb + 1) * P], dens[b][:, jb, :], ident[:])
-            joint[b] = keep.tile([P, S], F32, name="joint%d" % b)
-            nc.vector.tensor_tensor(out=joint[b][:], in0=e_ps[:], in1=post_sb[b][:], op=ALU.mult)
-            nc.gpsimd.tensor_tensor(out=grown[:, b, 1:S], in0=joint[b][:, 0:S - 1], in1=stay[:, 0:S - 1], op=ALU.mult)
+            nc.vector.tensor_tensor(out=joint[b][:, 1:S + 1], in0=e_ps[:], in1=post_sb[b][:], op=ALU.mult)
+
+        def grow(b):
+            grown[b] = keep.tile([P, S], F32, name="grown%d" % b, align_bytes=64)
+            nc.gpsimd.tensor_tensor(out=grown[b][:], in0=joint[b][:, 0:S], in1=stay[:, 0:S], op=ALU.mult)
 
         def change(b):
             stats[b] = keep.tile([P, 4], F32, name="stats%d" % b)
-            ch = keep.tile([P, S], F32, name="ch", tag="ch", bufs=2)
-            nc.vector.scalar_tensor_tensor(out=ch[:], in0=haz_ps[:], scalar=1.0, in1=joint[b][:],
+            ch = keep.tile([P, S], F32, name="ch%d" % b, tag=("joint2" if b == 3 else "ch%d" % b))
+            nc.vector.scalar_tensor_tensor(out=ch[:], in0=haz_ps[:], scalar=1.0, in1=joint[b][:, 1:S + 1],
                                            op0=ALU.mult, op1=ALU.mult, accum_out=stats[b][:, 0:1])
 
         def finish(b):
             weights[b] = keep.tile([P, S], F32, name="nw%d" % b)
-            nc.vector.scalar_tensor_tensor(out=weights[b][:], in0=start_ps[:], scalar=stats[b][:, 0:1], in1=grown[:, b, :],
+            nc.vector.scalar_tensor_tensor(out=weights[b][:], in0=start_ps[:], scalar=stats[b][:, 0:1], in1=grown[b][:],
                                            op0=ALU.mult, op1=ALU.add, accum_out=stats[b][:, 1:2])
 
         def invert(b):
@@ -204,16 +222,19 @@ def tile_picked_ybocpd_post_p_kernel(tc, x_words, x_scales, hT, norm, post, haz,
                                   x_win[1][:].bitcast(U32).indirect(offsets[:, half * 16:(half + 1) * 16]))
             mx_half(0, 1, half)
             exp_half(0, half)
-        cast_h(1, 0, nc.vector.tensor_copy)
-        quant_h(1, 0)
+        cast_h((2, 3), 0, nc.vector.tensor_copy,
+               over.tile([P, W, 4], BF16, name="h_bf20", align_bytes=64, offset=CAST_AT + 3 * HALF_ROW))
+        quant_h((2, 3), 0)
         turn(0)
         for half in range(2):
             mx_half(1, 1, half)
             exp_half(1, half)
+        grow(0)
         change(0)
         turn(1)
-        cast_h(1, 1, nc.scalar.copy)
-        quant_h(1, 1)
+        grow(1)
+        cast_h((2, 3), 1, nc.scalar.copy, keep.tile([P, W, 4], BF16, name="h_bf21", tag="dens0", align_bytes=64))
+        quant_h((2, 3), 1)
         for b in (2, 3):
             for half in range(2):
                 mx_half(b, 0, half)
@@ -223,6 +244,7 @@ def tile_picked_ybocpd_post_p_kernel(tc, x_words, x_scales, hT, norm, post, haz,
         change(1)
         finish(0)
         turn(2)
+        grow(2)
         for half in range(2):
             mx_half(3, 1, half)
             exp_half(3, half)
@@ -233,6 +255,7 @@ def tile_picked_ybocpd_post_p_kernel(tc, x_words, x_scales, hT, norm, post, haz,
         invert(1)
         normalise_scalar(1)
         turn(3)
+        grow(3)
         finish(2)
         change(3)
         invert(2)

@@ -30,6 +30,7 @@ WIN_BYTES = T * 4
 NORM_AT = WIN_BYTES + RAW_BYTES + HALF_ROW
 FIRST_AT = NORM_AT + WIN_BYTES
 CAST_AT = FIRST_AT + RAW_BYTES
+DENS_AT = CAST_AT + 3 * ROW_BYTES
 
 
 def tile_picked_ybocpd_post_p_kernel(tc, x_words, x_scales, hT, norm, post, haz, start, offs, out):
@@ -106,7 +107,7 @@ def tile_picked_ybocpd_post_p_kernel(tc, x_words, x_scales, hT, norm, post, haz,
         load_post(0, NORM_AT - HALF_ROW)
         load_post(1, NORM_AT + HALF_ROW + RAW_BYTES)
 
-        h_bf, h_codes, h_scales = {}, {}, {}
+        h_bf, h_quant = {}, {}
 
         def cast_h(blocks, g, copy, tile):
             c, first = blocks[0] // 2, (blocks[0] % 2) * P
@@ -120,9 +121,7 @@ def tile_picked_ybocpd_post_p_kernel(tc, x_words, x_scales, hT, norm, post, haz,
             scales = keep.tile([P, width], U8, name="h_scales%d%d" % (blocks[0], g), align_bytes=64)
             nc.vector.quantize_mx(out=codes[:].bitcast(FP8X4), scales=scales[:],
                                   in_=h_bf[blocks, g][:].rearrange("p w j -> p (w j)"))
-            for i, b in enumerate(blocks):
-                h_codes[b, g] = codes[:, i * P:(i + 1) * P]
-                h_scales[b, g] = scales[:, i * P:(i + 1) * P]
+            h_quant[blocks[0] // 2, g] = (codes, scales)
 
         for g in range(PASSES):
             cast_h((0, 1), g, nc.scalar.copy,
@@ -154,46 +153,47 @@ def tile_picked_ybocpd_post_p_kernel(tc, x_words, x_scales, hT, norm, post, haz,
 
         sums = {}
 
-        def mx_half(b, g, half):
+        def mx_pass(c, g, jb):
             if g == 0:
-                sums[b, half] = psum.tile([P, 2, P], F32, name="sums%d%d" % (b, half), tag="sums", bufs=4)
-            for u in range(2):
-                runs = slice((2 * half + u) * P, (2 * half + u + 1) * P)
-                nc.tensor.matmul_mx(out=sums[b, half][:, u, :], lhsT=x_pick[g][:, runs].bitcast(FP8X4),
-                                    lhsT_scale=s_plane[:, g * S + runs.start:g * S + runs.stop], rhs=h_codes[b, g].bitcast(FP8X4),
-                                    rhs_scale=h_scales[b, g],
-                                    start=(g == 0 and u == 0), stop=(g == PASSES - 1 and u == 1))
+                sums[c, jb] = psum.tile([P, W], F32, name="sums%d%d" % (c, jb), tag="sums%d" % jb)
+            codes, scales = h_quant[c, g]
+            nc.tensor.matmul_mx(out=sums[c, jb][:], lhsT=x_pick[g][:, jb * P:(jb + 1) * P].bitcast(FP8X4),
+                                lhsT_scale=s_plane[:, g * S + jb * P:g * S + (jb + 1) * P],
+                                rhs=codes[:].bitcast(FP8X4), rhs_scale=scales[:],
+                                start=(g == 0), stop=(g == PASSES - 1))
 
-        dens = {}
+        dens = (keep.tile([P, NB, W], F32, name="dens0"), over.tile([P, NB, W], F32, name="dens1", offset=DENS_AT))
 
-        def exp_half(b, half):
-            if half == 0:
-                dens[b] = keep.tile([P, NB, P], F32, name="dens%d" % b, align_bytes=64)
-            for u in range(2):
-                jb = 2 * half + u
-                nc.scalar.activation(out=dens[b][:, jb, :], in_=sums[b, half][:, u, :], func=ACT.Exp,
-                                     bias=bias[:, jb:jb + 1], scale=0.7)
+        def exp_of(c, jb, lo, hi):
+            nc.scalar.activation(out=dens[c][:, jb, lo:hi], in_=sums[c, jb][:, lo:hi], func=ACT.Exp,
+                                 bias=bias[:, jb:jb + 1], scale=0.7)
 
         grown, stats, weights = {}, {}, {}
 
         def turn(b):
             e_ps = psum.tile([P, S], F32, name="e_ps%d" % b, tag="turn", bufs=2)
             for jb in range(NB):
-                nc.tensor.transpose(e_ps[:, jb * P:(jb + 1) * P], dens[b][:, jb, :], ident[:])
+                nc.tensor.transpose(e_ps[:, jb * P:(jb + 1) * P], dens[b // 2][:, jb, (b % 2) * P:(b % 2 + 1) * P], ident[:])
             nc.vector.tensor_tensor(out=joint[b][:, 1:S + 1], in0=e_ps[:], in1=post_sb[b][:], op=ALU.mult)
 
         def grow(b):
-            grown[b] = keep.tile([P, S], F32, name="grown%d" % b, align_bytes=64)
+            grown[b] = keep.tile([P, S], F32, name="grown%d" % b, tag=("h_bf21" if b == 0 else "grown%d" % b), align_bytes=64)
             nc.gpsimd.tensor_tensor(out=grown[b][:], in0=joint[b][:, 0:S], in1=stay[:, 0:S], op=ALU.mult)
 
         def change(b):
             stats[b] = keep.tile([P, 4], F32, name="stats%d" % b)
-            ch = keep.tile([P, S], F32, name="ch%d" % b, tag=("joint2" if b == 3 else "ch%d" % b))
+            if b == 2:
+                ch = over.tile([P, S], F32, name="ch2", offset=DENS_AT)
+            else:
+                ch = keep.tile([P, S], F32, name="ch%d" % b)
             nc.vector.scalar_tensor_tensor(out=ch[:], in0=haz_ps[:], scalar=1.0, in1=joint[b][:, 1:S + 1],
                                            op0=ALU.mult, op1=ALU.mult, accum_out=stats[b][:, 0:1])
 
         def finish(b):
-            weights[b] = keep.tile([P, S], F32, name="nw%d" % b)
+            if b == 1:
+                weights[b] = over.tile([P, S], F32, name="nw1", offset=DENS_AT + ROW_BYTES)
+            else:
+                weights[b] = keep.tile([P, S], F32, name="nw%d" % b)
             nc.vector.scalar_tensor_tensor(out=weights[b][:], in0=start_ps[:], scalar=stats[b][:, 0:1], in1=grown[b][:],
                                            op0=ALU.mult, op1=ALU.add, accum_out=stats[b][:, 1:2])
 
@@ -213,49 +213,44 @@ def tile_picked_ybocpd_post_p_kernel(tc, x_words, x_scales, hT, norm, post, haz,
                 nc.vector.tensor_scalar(res[:, cols], weights[b][:, cols], stats[b][:, 2:3], 100.0, ALU.mult, ALU.mult)
                 queue.dma_start(out=out[b * P:(b + 1) * P, cols], in_=res[:, cols])
 
-        for b in range(2):
-            for half in range(2):
-                mx_half(b, 0, half)
+        for jb in range(NB):
+            mx_pass(0, 0, jb)
         x_pick[1] = over.tile([P, S], U32, name="x_pick1", align_bytes=64, offset=CAST_AT + HALF_ROW)
         for half in range(2):
             nc.vector.tensor_copy(x_pick[1][:, half * 256:(half + 1) * 256],
                                   x_win[1][:].bitcast(U32).indirect(offsets[:, half * 16:(half + 1) * 16]))
-            mx_half(0, 1, half)
-            exp_half(0, half)
+            for jb in (2 * half, 2 * half + 1):
+                mx_pass(0, 1, jb)
+                exp_of(0, jb, 0, P if half else W)
         cast_h((2, 3), 0, nc.vector.tensor_copy,
                over.tile([P, W, 4], BF16, name="h_bf20", align_bytes=64, offset=CAST_AT + 3 * HALF_ROW))
         quant_h((2, 3), 0)
+        cast_h((2, 3), 1, nc.vector.tensor_copy, keep.tile([P, W, 4], BF16, name="h_bf21", align_bytes=64))
+        quant_h((2, 3), 1)
         turn(0)
-        for half in range(2):
-            mx_half(1, 1, half)
-            exp_half(1, half)
         grow(0)
-        change(0)
+        for jb in (2, 3):
+            exp_of(0, jb, P, W)
         turn(1)
         grow(1)
-        cast_h((2, 3), 1, nc.scalar.copy, keep.tile([P, W, 4], BF16, name="h_bf21", tag="dens0", align_bytes=64))
-        quant_h((2, 3), 1)
-        for b in (2, 3):
-            for half in range(2):
-                mx_half(b, 0, half)
-        for half in range(2):
-            mx_half(2, 1, half)
-            exp_half(2, half)
+        for g in range(PASSES):
+            for jb in range(NB):
+                mx_pass(1, g, jb)
+        for jb in range(NB):
+            exp_of(1, jb, 0, W)
+        change(0)
         change(1)
-        finish(0)
         turn(2)
         grow(2)
-        for half in range(2):
-            mx_half(3, 1, half)
-            exp_half(3, half)
+        finish(0)
+        turn(3)
+        grow(3)
         invert(0)
         normalise_scalar(0)
         finish(1)
         change(2)
         invert(1)
         normalise_scalar(1)
-        turn(3)
-        grow(3)
         finish(2)
         change(3)
         invert(2)

@@ -130,10 +130,20 @@ def tile_picked_ybocpd_post_p_kernel(tc, x_words, x_scales, hT, norm, post, haz,
         load_post(2, FIRST_AT)
         load_post(3, FIRST_AT + ROW_BYTES)
 
-        hs_ps = psum.tile([P, P], F32, name="hs_ps", tag="turn", bufs=2)
-        nc.tensor.transpose(hs_ps[:], hs_rows[:], ident[:])
+        is_last = ident[:, P - 1:P]
+        not_last = keep.tile([P, 1], F32, name="not_last")
+        nc.scalar.activation(out=not_last[:], in_=is_last, func=ACT.Identity, scale=-1.0, bias=one[:])
+        hs_ps = psum.tile([P, 2, P], F32, name="hs_ps", tag="turn", bufs=2)
+        nc.tensor.transpose(hs_ps[:, 0, :], hs_rows[:], ident[:])
+        nc.tensor.transpose(hs_ps[:, 1, :], hs_rows[:, P - 1:P].to_broadcast([P, P]), ident[:])
         hs_cols = keep.tile([P, 2 * NB], F32, name="hs_cols")
-        nc.scalar.copy(out=hs_cols[:], in_=hs_ps[:, HS_ROW:P])
+        last_haz = HS_ROW + NB - 1
+        nc.scalar.copy(out=hs_cols[:, 0:NB - 1], in_=hs_ps[:, 0, HS_ROW:last_haz])
+        nc.scalar.activation(out=hs_cols[:, NB - 1:NB], in_=hs_ps[:, 0, last_haz:last_haz + 1], func=ACT.Identity,
+                             scale=not_last[:], bias=is_last)
+        nc.scalar.activation(out=hs_cols[:, NB:2 * NB], in_=hs_ps[:, 0, last_haz + 1:P], func=ACT.Copy, scale=100.0)
+        haz_end = keep.tile([P, 1], F32, name="haz_end")
+        nc.scalar.copy(out=haz_end[:], in_=hs_ps[:, 1, last_haz:last_haz + 1])
         haz_ps = psum.tile([P, S], F32, name="haz_ps")
         start_ps = psum.tile([P, S], F32, name="start_ps")
         for a, bank in enumerate((haz_ps, start_ps)):
@@ -145,7 +155,12 @@ def tile_picked_ybocpd_post_p_kernel(tc, x_words, x_scales, hT, norm, post, haz,
             nc.tensor.transpose(n_ps[:, jb, :], n_pick[:, jb * P:(jb + 1) * P], ident[:])
         bias = keep.tile([P, NB], F32, name="bias")
         nc.scalar.copy(out=bias[:], in_=n_ps[:, :, NORM_ROW])
-        nc.scalar.activation(out=stay[:, 1:S + 1], in_=haz_ps[:], func=ACT.Identity, scale=-1.0, bias=one[:])
+        nc.scalar.activation(out=stay[:, 1:S + 1], in_=haz_ps[:], func=ACT.Copy, scale=-100.0, bias=100.0)
+        start_sb = keep.tile([P, S], F32, name="start_sb")
+        start_sum = keep.tile([P, 1], F32, name="start_sum")
+        nc.scalar.activation(out=start_sb[:], in_=start_ps[:], func=ACT.Copy, accum_out=start_sum[:])
+        excess = keep.tile([P, 1], F32, name="excess")
+        nc.scalar.activation(out=excess[:], in_=start_sum[:], func=ACT.Copy, scale=0.01, bias=-1.0)
 
         x_pick = {}
         x_pick[0] = keep.tile([P, S], U32, name="x_pick0", align_bytes=64)
@@ -168,50 +183,52 @@ def tile_picked_ybocpd_post_p_kernel(tc, x_words, x_scales, hT, norm, post, haz,
             nc.scalar.activation(out=dens[c][:, jb, lo:hi], in_=sums[c, jb][:, lo:hi], func=ACT.Exp,
                                  bias=bias[:, jb:jb + 1], scale=0.7)
 
-        grown, stats, weights = {}, {}, {}
+        grown, sums_v, sums_s, scaled = {}, {}, {}, {}
+
+        def fold_end(b):
+            nc.scalar.activation(out=post_sb[b][:, S - 1:S], in_=post_sb[b][:, S - 1:S], func=ACT.Copy, scale=haz_end[:])
 
         def turn(b):
             e_ps = psum.tile([P, S], F32, name="e_ps%d" % b, tag="turn", bufs=2)
             for jb in range(NB):
                 nc.tensor.transpose(e_ps[:, jb * P:(jb + 1) * P], dens[b // 2][:, jb, (b % 2) * P:(b % 2 + 1) * P], ident[:])
-            nc.vector.tensor_tensor(out=joint[b][:, 1:S + 1], in0=e_ps[:], in1=post_sb[b][:], op=ALU.mult)
+            sums_v[b] = keep.tile([P, 3], F32, name="sums_v%d" % b)
+            nc.vector.scalar_tensor_tensor(out=joint[b][:, 1:S + 1], in0=e_ps[:], scalar=1.0, in1=post_sb[b][:],
+                                           op0=ALU.mult, op1=ALU.mult, accum_out=sums_v[b][:, 0:1])
 
         def grow(b):
             grown[b] = keep.tile([P, S], F32, name="grown%d" % b, tag=("h_bf21" if b == 0 else "grown%d" % b), align_bytes=64)
             nc.gpsimd.tensor_tensor(out=grown[b][:], in0=joint[b][:, 0:S], in1=stay[:, 0:S], op=ALU.mult)
 
         def change(b):
-            stats[b] = keep.tile([P, 4], F32, name="stats%d" % b)
             if b == 2:
-                ch = over.tile([P, S], F32, name="ch2", offset=DENS_AT)
+                ch = over.tile([P, S], F32, name="ch2", offset=DENS_AT - HALF_ROW)
             else:
                 ch = keep.tile([P, S], F32, name="ch%d" % b)
             nc.vector.scalar_tensor_tensor(out=ch[:], in0=haz_ps[:], scalar=1.0, in1=joint[b][:, 1:S + 1],
-                                           op0=ALU.mult, op1=ALU.mult, accum_out=stats[b][:, 0:1])
-
-        def finish(b):
-            if b == 1:
-                weights[b] = over.tile([P, S], F32, name="nw1", offset=DENS_AT + ROW_BYTES)
-            else:
-                weights[b] = keep.tile([P, S], F32, name="nw%d" % b)
-            nc.vector.scalar_tensor_tensor(out=weights[b][:], in0=start_ps[:], scalar=stats[b][:, 0:1], in1=grown[b][:],
-                                           op0=ALU.mult, op1=ALU.add, accum_out=stats[b][:, 1:2])
+                                           op0=ALU.mult, op1=ALU.mult, accum_out=sums_v[b][:, 1:2])
+            sums_s[b] = keep.tile([P, 2], F32, name="sums_s%d" % b)
+            nc.scalar.activation(out=sums_s[b][:, 0:1], in_=sums_v[b][:, 1:2], func=ACT.Identity,
+                                 scale=excess[:], bias=sums_v[b][:, 0:1])
 
         def invert(b):
-            nc.vector.reciprocal(out=stats[b][:, 2:3], in_=stats[b][:, 1:2])
+            nc.vector.reciprocal(out=sums_v[b][:, 2:3], in_=sums_s[b][:, 0:1])
+            nc.scalar.activation(out=sums_s[b][:, 1:2], in_=sums_v[b][:, 1:2], func=ACT.Copy, scale=sums_v[b][:, 2:3])
+            scaled[b] = keep.tile([P, S], F32, name="scaled%d" % b)
+            nc.scalar.activation(out=scaled[b][:], in_=grown[b][:], func=ACT.Copy, scale=sums_v[b][:, 2:3])
 
-        def normalise_scalar(b):
-            res = keep.tile([P, S], F32, name="res%d" % b)
-            factor = keep.tile([P, 1], F32, name="factor%d" % b)
-            nc.scalar.activation(out=factor[:], in_=stats[b][:, 2:3], func=ACT.Copy, scale=100.0)
-            nc.scalar.activation(out=res[:], in_=weights[b][:], func=ACT.Copy, scale=factor[:])
-            nc.sync.dma_start(out=out[b * P:(b + 1) * P, :], in_=res[:])
-
-        def normalise_vector(b):
-            res = keep.tile([P, S], F32, name="res%d" % b)
-            for cols, queue in ((slice(0, S // 2), nc.sync), (slice(S // 2, S), nc.scalar)):
-                nc.vector.tensor_scalar(res[:, cols], weights[b][:, cols], stats[b][:, 2:3], 100.0, ALU.mult, ALU.mult)
+        def finish(b, pieces):
+            if b < 2:
+                res = over.tile([P, S], F32, name="res%d" % b, offset=DENS_AT + HALF_ROW + b * ROW_BYTES)
+            else:
+                res = keep.tile([P, S], F32, name="res%d" % b)
+            for cols, queue in pieces:
+                nc.vector.scalar_tensor_tensor(out=res[:, cols], in0=start_ps[:, cols], scalar=sums_s[b][:, 1:2],
+                                               in1=scaled[b][:, cols], op0=ALU.mult, op1=ALU.add)
                 queue.dma_start(out=out[b * P:(b + 1) * P, cols], in_=res[:, cols])
+
+        whole = ((slice(0, S), nc.sync),)
+        halves = ((slice(0, S // 2), nc.sync), (slice(S // 2, S), nc.scalar))
 
         for jb in range(NB):
             mx_pass(0, 0, jb)
@@ -227,10 +244,13 @@ def tile_picked_ybocpd_post_p_kernel(tc, x_words, x_scales, hT, norm, post, haz,
         quant_h((2, 3), 0)
         cast_h((2, 3), 1, nc.vector.tensor_copy, keep.tile([P, W, 4], BF16, name="h_bf21", align_bytes=64))
         quant_h((2, 3), 1)
+        fold_end(0)
         turn(0)
         grow(0)
         for jb in (2, 3):
             exp_of(0, jb, P, W)
+        for b in range(1, NB):
+            fold_end(b)
         turn(1)
         grow(1)
         for g in range(PASSES):
@@ -240,21 +260,17 @@ def tile_picked_ybocpd_post_p_kernel(tc, x_words, x_scales, hT, norm, post, haz,
             exp_of(1, jb, 0, W)
         change(0)
         change(1)
+        invert(0)
         turn(2)
         grow(2)
-        finish(0)
+        invert(1)
         turn(3)
         grow(3)
-        invert(0)
-        normalise_scalar(0)
-        finish(1)
         change(2)
-        invert(1)
-        normalise_scalar(1)
-        finish(2)
         change(3)
         invert(2)
-        normalise_scalar(2)
-        finish(3)
+        finish(0, whole)
         invert(3)
-        normalise_vector(3)
+        finish(1, whole)
+        finish(2, whole)
+        finish(3, halves)

@@ -109,24 +109,27 @@ def tile_picked_ybocpd_post_p_kernel(tc, x_words, x_scales, hT, norm, post, haz,
 
         h_bf, h_quant = {}, {}
 
-        def cast_h(blocks, g, copy, tile):
-            c, first = blocks[0] // 2, (blocks[0] % 2) * P
-            h_bf[blocks, g] = tile
-            copy(out=tile[:].rearrange("p (c i) t -> p c t i", i=4),
-                 in_=h_raw[c, g][:, :, first:first + P * len(blocks)].rearrange("p t (c i) -> p c t i", i=4))
+        def cast_h(c, g, copy, tile, pieces):
+            h_bf[c, g] = tile
+            for lo, hi in pieces:
+                copy(out=tile[:, lo:hi, :].rearrange("p (c i) t -> p c t i", i=4),
+                     in_=h_raw[c, g][:, :, lo:hi].rearrange("p t (c i) -> p c t i", i=4))
 
-        def quant_h(blocks, g):
-            width = P * len(blocks)
-            codes = keep.tile([P, width], U32, name="h_codes%d%d" % (blocks[0], g), align_bytes=64)
-            scales = keep.tile([P, width], U8, name="h_scales%d%d" % (blocks[0], g), align_bytes=64)
-            nc.vector.quantize_mx(out=codes[:].bitcast(FP8X4), scales=scales[:],
-                                  in_=h_bf[blocks, g][:].rearrange("p w j -> p (w j)"))
-            h_quant[blocks[0] // 2, g] = (codes, scales)
+        def quant_h(c, g, pieces):
+            codes = keep.tile([P, W], U32, name="h_codes%d%d" % (c, g), align_bytes=64)
+            scales = keep.tile([P, W], U8, name="h_scales%d%d" % (c, g), align_bytes=64)
+            for lo, hi in pieces:
+                nc.vector.quantize_mx(out=codes[:, lo:hi].bitcast(FP8X4), scales=scales[:, lo:hi],
+                                      in_=h_bf[c, g][:, lo:hi, :].rearrange("p w j -> p (w j)"))
+            h_quant[c, g] = (codes, scales)
+
+        at_once = ((0, W),)
+        by_block = ((0, P), (P, W))
 
         for g in range(PASSES):
-            cast_h((0, 1), g, nc.scalar.copy,
-                   over.tile([P, W, 4], BF16, name="h_bf0%d" % g, align_bytes=64, offset=CAST_AT + g * ROW_BYTES))
-            quant_h((0, 1), g)
+            cast_h(0, g, nc.scalar.copy,
+                   over.tile([P, W, 4], BF16, name="h_bf0%d" % g, align_bytes=64, offset=CAST_AT + g * ROW_BYTES), at_once)
+            quant_h(0, g, at_once)
         load_post(2, FIRST_AT)
         load_post(3, FIRST_AT + ROW_BYTES)
 
@@ -239,11 +242,11 @@ def tile_picked_ybocpd_post_p_kernel(tc, x_words, x_scales, hT, norm, post, haz,
             for jb in (2 * half, 2 * half + 1):
                 mx_pass(0, 1, jb)
                 exp_of(0, jb, 0, P if half else W)
-        cast_h((2, 3), 0, nc.vector.tensor_copy,
-               over.tile([P, W, 4], BF16, name="h_bf20", align_bytes=64, offset=CAST_AT + 3 * HALF_ROW))
-        quant_h((2, 3), 0)
-        cast_h((2, 3), 1, nc.vector.tensor_copy, keep.tile([P, W, 4], BF16, name="h_bf21", align_bytes=64))
-        quant_h((2, 3), 1)
+        cast_h(1, 0, nc.vector.tensor_copy,
+               over.tile([P, W, 4], BF16, name="h_bf20", align_bytes=64, offset=CAST_AT + 3 * HALF_ROW), by_block)
+        quant_h(1, 0, by_block)
+        cast_h(1, 1, nc.vector.tensor_copy, keep.tile([P, W, 4], BF16, name="h_bf21", align_bytes=64), by_block)
+        quant_h(1, 1, by_block)
         fold_end(0)
         turn(0)
         grow(0)
@@ -257,12 +260,14 @@ def tile_picked_ybocpd_post_p_kernel(tc, x_words, x_scales, hT, norm, post, haz,
             for jb in range(NB):
                 mx_pass(1, g, jb)
         for jb in range(NB):
-            exp_of(1, jb, 0, W)
+            exp_of(1, jb, 0, W if jb < 2 else P)
         change(0)
         change(1)
         invert(0)
         turn(2)
         grow(2)
+        for jb in (2, 3):
+            exp_of(1, jb, P, W)
         invert(1)
         turn(3)
         grow(3)

@@ -27,10 +27,17 @@ RAW_BYTES = 4 * W * 4
 ROW_BYTES = S * 4
 HALF_ROW = ROW_BYTES // 2
 WIN_BYTES = T * 4
-NORM_AT = WIN_BYTES + RAW_BYTES + HALF_ROW
-FIRST_AT = NORM_AT + WIN_BYTES
-CAST_AT = FIRST_AT + RAW_BYTES
-DENS_AT = CAST_AT + 3 * ROW_BYTES
+LAP = 512
+SCALE_AT = RAW_BYTES - LAP
+PICK0_AT = SCALE_AT + T - LAP
+CAST0_AT = PICK0_AT + ROW_BYTES
+X0_AT = CAST0_AT + ROW_BYTES - LAP
+X1_AT = X0_AT + LAP + 2 * RAW_BYTES
+POST_AT = X1_AT + HALF_ROW
+RAW0_AT = POST_AT + NB * ROW_BYTES
+NPICK_AT = RAW0_AT + RAW_BYTES
+START_AT = NPICK_AT + ROW_BYTES
+DENS_AT = START_AT + ROW_BYTES + HALF_ROW
 
 
 def tile_picked_ybocpd_post_p_kernel(tc, x_words, x_scales, hT, norm, post, haz, start, offs, out):
@@ -63,18 +70,17 @@ def tile_picked_ybocpd_post_p_kernel(tc, x_words, x_scales, hT, norm, post, haz,
 
         offsets = keep.tile([P, S // 16], U16, name="offsets")
         nc.sync.dma_start(offsets[:], offs)
-        s_win = over.tile([P, T], U8, name="s_win", offset=WIN_BYTES - T // 2)
+        s_win = over.tile([P, T], U8, name="s_win", offset=SCALE_AT)
         nc.sync.dma_start(out=s_win[PARK:P, :].bitcast(I32),
-                            in_=x_scales.bitcast(I32).rearrange("g m n -> m g n"))
-        load_h(0, 0, keep.tile([P, 4, W], F32, name="h_raw00"))
-        n_win = over.tile([P, T], F32, name="n_win", offset=NORM_AT)
-        nc.sync.dma_start(out=n_win[NORM_ROW:P, :], in_=norm[0:1, :])
+                          in_=x_scales.bitcast(I32).rearrange("g m n -> m g n"))
+        load_x(0, over.tile([P, T], I32, name="x_win0", offset=X0_AT))
+        n_win = keep.tile([P, T], F32, name="n_win")
+        nc.scalar.dma_start(out=n_win[NORM_ROW:P, :], in_=norm[0:1, :])
         hs_rows = keep.tile([P, P], F32, name="hs_rows")
-        nc.sync.dma_start(out=hs_rows[HS_ROW:HS_ROW + NB, :], in_=haz[0:1, :].rearrange("r (b p) -> (r b) p", p=P))
-        nc.sync.dma_start(out=hs_rows[HS_ROW + NB:P, :], in_=start[0:1, :].rearrange("r (b p) -> (r b) p", p=P))
-
-        load_h(0, 1, over.tile([P, 4, W], F32, name="h_raw01", offset=FIRST_AT))
-        load_x(0, keep.tile([P, T], I32, name="x_win0", align_bytes=64))
+        nc.scalar.dma_start(out=hs_rows[HS_ROW:HS_ROW + NB, :], in_=haz[0:1, :].rearrange("r (b p) -> (r b) p", p=P))
+        nc.scalar.dma_start(out=hs_rows[HS_ROW + NB:P, :], in_=start[0:1, :].rearrange("r (b p) -> (r b) p", p=P))
+        load_h(0, 0, over.tile([P, 4, W], F32, name="h_raw00", offset=RAW0_AT))
+        load_x(1, over.tile([P, T], I32, name="x_win1", offset=X1_AT))
 
         joint = {}
         for b in range(NB):
@@ -98,40 +104,37 @@ def tile_picked_ybocpd_post_p_kernel(tc, x_words, x_scales, hT, norm, post, haz,
         for q in range(4):
             nc.sync.dma_start(out=s_plane[32 * q:32 * q + 4, :].bitcast(I32).rearrange("r (g n) -> r g n", g=PASSES),
                                 in_=s_pick[PARK + 8 * q:PARK + 8 * q + 8, :].bitcast(I32))
-        load_x(1, over.tile([P, T], I32, name="x_win1", offset=0))
-        load_h(1, 0, over.tile([P, 4, W], F32, name="h_raw10", offset=WIN_BYTES))
+        load_h(0, 1, over.tile([P, 4, W], F32, name="h_raw01", offset=0))
 
-        n_pick = keep.tile([P, S], F32, name="n_pick")
-        nc.vector.tensor_scalar(n_pick[:], n_win[:].indirect(offsets[:]), -0.7, 0.0, ALU.mult, ALU.add)
-        load_h(1, 1, over.tile([P, 4, W], F32, name="h_raw11", offset=NORM_AT + HALF_ROW))
-        load_post(0, NORM_AT - HALF_ROW)
-        load_post(1, NORM_AT + HALF_ROW + RAW_BYTES)
+        x_pick = {}
+
+        def pick_x(g, at):
+            x_pick[g] = over.tile([P, S], U32, name="x_pick%d" % g, align_bytes=64, offset=at)
+            nc.vector.tensor_copy(x_pick[g][:], x_win[g][:].bitcast(U32).indirect(offsets[:]))
+
+        pick_x(0, PICK0_AT)
+        for g in range(PASSES):
+            load_h(1, g, over.tile([P, 4, W], F32, name="h_raw1%d" % g, offset=X0_AT + LAP + g * RAW_BYTES))
+
+        n_pick = over.tile([P, S], F32, name="n_pick", offset=NPICK_AT)
+        nc.scalar.activation(out=n_pick[:], in_=n_win[:].indirect(offsets[:]), func=ACT.Copy)
 
         h_bf, h_quant = {}, {}
 
-        def cast_h(c, g, copy, tile, pieces):
-            h_bf[c, g] = tile
-            for lo, hi in pieces:
-                copy(out=tile[:, lo:hi, :].rearrange("p (c i) t -> p c t i", i=4),
-                     in_=h_raw[c, g][:, :, lo:hi].rearrange("p t (c i) -> p c t i", i=4))
+        def cast_h(c, g, half, copy, at):
+            tile = over.tile([P, P, 4], BF16, name="h_bf%d%d%d" % (c, g, half), align_bytes=64, offset=at)
+            h_bf[c, g, half] = tile
+            copy(out=tile[:].rearrange("p (c i) t -> p c t i", i=4),
+                 in_=h_raw[c, g][:, :, half * P:(half + 1) * P].rearrange("p t (c i) -> p c t i", i=4))
 
-        def quant_h(c, g, pieces):
-            codes = keep.tile([P, W], U32, name="h_codes%d%d" % (c, g), align_bytes=64)
-            scales = keep.tile([P, W], U8, name="h_scales%d%d" % (c, g), align_bytes=64)
-            for lo, hi in pieces:
-                nc.vector.quantize_mx(out=codes[:, lo:hi].bitcast(FP8X4), scales=scales[:, lo:hi],
-                                      in_=h_bf[c, g][:, lo:hi, :].rearrange("p w j -> p (w j)"))
-            h_quant[c, g] = (codes, scales)
-
-        at_once = ((0, W),)
-        by_block = ((0, P), (P, W))
-
-        for g in range(PASSES):
-            cast_h(0, g, nc.scalar.copy,
-                   over.tile([P, W, 4], BF16, name="h_bf0%d" % g, align_bytes=64, offset=CAST_AT + g * ROW_BYTES), at_once)
-            quant_h(0, g, at_once)
-        load_post(2, FIRST_AT)
-        load_post(3, FIRST_AT + ROW_BYTES)
+        def quant_h(c, g, half):
+            if half == 0:
+                h_quant[c, g] = (keep.tile([P, W], U32, name="h_codes%d%d" % (c, g), align_bytes=64),
+                                 keep.tile([P, W], U8, name="h_scales%d%d" % (c, g), align_bytes=64))
+            codes, scales = h_quant[c, g]
+            cols = slice(half * P, (half + 1) * P)
+            nc.vector.quantize_mx(out=codes[:, cols].bitcast(FP8X4), scales=scales[:, cols],
+                                  in_=h_bf[c, g, half][:].rearrange("p w j -> p (w j)"))
 
         is_last = ident[:, P - 1:P]
         not_last = keep.tile([P, 1], F32, name="not_last")
@@ -157,17 +160,13 @@ def tile_picked_ybocpd_post_p_kernel(tc, x_words, x_scales, hT, norm, post, haz,
         for jb in range(NB):
             nc.tensor.transpose(n_ps[:, jb, :], n_pick[:, jb * P:(jb + 1) * P], ident[:])
         bias = keep.tile([P, NB], F32, name="bias")
-        nc.scalar.copy(out=bias[:], in_=n_ps[:, :, NORM_ROW])
+        nc.scalar.activation(out=bias[:], in_=n_ps[:, :, NORM_ROW], func=ACT.Copy, scale=-0.7)
         nc.scalar.activation(out=stay[:, 1:S + 1], in_=haz_ps[:], func=ACT.Copy, scale=-100.0, bias=100.0)
-        start_sb = keep.tile([P, S], F32, name="start_sb")
+        start_sb = over.tile([P, S], F32, name="start_sb", offset=START_AT)
         start_sum = keep.tile([P, 1], F32, name="start_sum")
         nc.scalar.activation(out=start_sb[:], in_=start_ps[:], func=ACT.Copy, accum_out=start_sum[:])
         excess = keep.tile([P, 1], F32, name="excess")
         nc.scalar.activation(out=excess[:], in_=start_sum[:], func=ACT.Copy, scale=0.01, bias=-1.0)
-
-        x_pick = {}
-        x_pick[0] = keep.tile([P, S], U32, name="x_pick0", align_bytes=64)
-        nc.vector.tensor_copy(x_pick[0][:], x_win[0][:].bitcast(U32).indirect(offsets[:]))
 
         sums = {}
 
@@ -200,7 +199,10 @@ def tile_picked_ybocpd_post_p_kernel(tc, x_words, x_scales, hT, norm, post, haz,
                                            op0=ALU.mult, op1=ALU.mult, accum_out=sums_v[b][:, 0:1])
 
         def grow(b):
-            grown[b] = keep.tile([P, S], F32, name="grown%d" % b, tag=("h_bf21" if b == 0 else "grown%d" % b), align_bytes=64)
+            if b == 0:
+                grown[b] = over.tile([P, S], F32, name="grown0", offset=X0_AT + LAP + HALF_ROW)
+            else:
+                grown[b] = keep.tile([P, S], F32, name="grown%d" % b)
             nc.gpsimd.tensor_tensor(out=grown[b][:], in0=joint[b][:, 0:S], in1=stay[:, 0:S], op=ALU.mult)
 
         def change(b):
@@ -233,20 +235,27 @@ def tile_picked_ybocpd_post_p_kernel(tc, x_words, x_scales, hT, norm, post, haz,
         whole = ((slice(0, S), nc.sync),)
         halves = ((slice(0, S // 2), nc.sync), (slice(S // 2, S), nc.scalar))
 
+        for g in range(PASSES):
+            if g == 0:
+                cast_h(0, 0, 1, nc.vector.tensor_copy, CAST0_AT + HALF_ROW)
+                cast_h(0, 0, 0, nc.vector.tensor_copy, SCALE_AT + LAP)
+            else:
+                pick_x(1, RAW0_AT)
+                for b in range(NB):
+                    load_post(b, POST_AT + b * ROW_BYTES)
+                cast_h(0, 1, 0, nc.vector.tensor_copy, X1_AT)
+                cast_h(0, 1, 1, nc.scalar.copy, START_AT - LAP)
+            for half in range(2):
+                quant_h(0, g, half)
+            for jb in range(NB):
+                mx_pass(0, g, jb)
         for jb in range(NB):
-            mx_pass(0, 0, jb)
-        x_pick[1] = over.tile([P, S], U32, name="x_pick1", align_bytes=64, offset=CAST_AT + HALF_ROW)
-        for half in range(2):
-            nc.vector.tensor_copy(x_pick[1][:, half * 256:(half + 1) * 256],
-                                  x_win[1][:].bitcast(U32).indirect(offsets[:, half * 16:(half + 1) * 16]))
-            for jb in (2 * half, 2 * half + 1):
-                mx_pass(0, 1, jb)
-                exp_of(0, jb, 0, P if half else W)
-        cast_h(1, 0, nc.vector.tensor_copy,
-               over.tile([P, W, 4], BF16, name="h_bf20", align_bytes=64, offset=CAST_AT + 3 * HALF_ROW), by_block)
-        quant_h(1, 0, by_block)
-        cast_h(1, 1, nc.vector.tensor_copy, keep.tile([P, W, 4], BF16, name="h_bf21", align_bytes=64), by_block)
-        quant_h(1, 1, by_block)
+            exp_of(0, jb, 0, W if jb < 2 else P)
+        for g, at in enumerate((0, X0_AT + LAP)):
+            for half in range(2):
+                cast_h(1, g, half, nc.vector.tensor_copy, at + half * HALF_ROW)
+            for half in range(2):
+                quant_h(1, g, half)
         fold_end(0)
         turn(0)
         grow(0)

@@ -188,7 +188,11 @@ def tile_picked_ybocpd_post_p_kernel(tc, x_words, x_scales, hT, norm, post, haz,
         grown, sums_v, sums_s, scaled = {}, {}, {}, {}
 
         def fold_end(b):
-            nc.scalar.activation(out=post_sb[b][:, S - 1:S], in_=post_sb[b][:, S - 1:S], func=ACT.Copy, scale=haz_end[:])
+            last = post_sb[b][:, S - 1:S]
+            if b == 0:
+                nc.vector.tensor_scalar(last, last, haz_end[:], None, ALU.mult)
+            else:
+                nc.scalar.activation(out=last, in_=last, func=ACT.Copy, scale=haz_end[:])
 
         def turn(b):
             e_ps = psum.tile([P, S], F32, name="e_ps%d" % b, tag="turn", bufs=2)
@@ -242,7 +246,7 @@ def tile_picked_ybocpd_post_p_kernel(tc, x_words, x_scales, hT, norm, post, haz,
             else:
                 pick_x(1, RAW0_AT)
                 for b in range(NB):
-                    load_post(b, POST_AT + b * ROW_BYTES)
+                    load_post(b, POST_AT + b * ROW_BYTES if b else RAW0_AT + ROW_BYTES)
                 cast_h(0, 1, 0, nc.vector.tensor_copy, X1_AT)
                 cast_h(0, 1, 1, nc.scalar.copy, START_AT - LAP)
             for half in range(2):
@@ -254,9 +258,10 @@ def tile_picked_ybocpd_post_p_kernel(tc, x_words, x_scales, hT, norm, post, haz,
         for g, at in enumerate((0, X0_AT + LAP)):
             for half in range(2):
                 cast_h(1, g, half, nc.vector.tensor_copy, at + half * HALF_ROW)
-            for half in range(2):
-                quant_h(1, g, half)
-        fold_end(0)
+            quant_h(1, g, 0)
+            if g == 1:
+                fold_end(0)
+            quant_h(1, g, 1)
         turn(0)
         grow(0)
         for jb in (2, 3):

@@ -35,9 +35,7 @@ X0_AT = CAST0_AT + ROW_BYTES - LAP
 X1_AT = X0_AT + LAP + 2 * RAW_BYTES
 POST_AT = X1_AT + HALF_ROW
 RAW0_AT = POST_AT + NB * ROW_BYTES
-NPICK_AT = RAW0_AT + RAW_BYTES
-START_AT = NPICK_AT + ROW_BYTES
-DENS_AT = START_AT + ROW_BYTES + HALF_ROW
+DENS_AT = RAW0_AT + RAW_BYTES + HALF_ROW
 
 
 def tile_picked_ybocpd_post_p_kernel(tc, x_words, x_scales, hT, norm, post, haz, start, offs, out):
@@ -116,7 +114,7 @@ def tile_picked_ybocpd_post_p_kernel(tc, x_words, x_scales, hT, norm, post, haz,
         for g in range(PASSES):
             load_h(1, g, over.tile([P, 4, W], F32, name="h_raw1%d" % g, offset=X0_AT + LAP + g * RAW_BYTES))
 
-        n_pick = over.tile([P, S], F32, name="n_pick", offset=NPICK_AT)
+        n_pick = keep.tile([P, S], F32, name="n_pick")
         nc.scalar.activation(out=n_pick[:], in_=n_win[:].indirect(offsets[:]), func=ACT.Copy)
 
         h_bf, h_quant = {}, {}
@@ -162,7 +160,7 @@ def tile_picked_ybocpd_post_p_kernel(tc, x_words, x_scales, hT, norm, post, haz,
         bias = keep.tile([P, NB], F32, name="bias")
         nc.scalar.activation(out=bias[:], in_=n_ps[:, :, NORM_ROW], func=ACT.Copy, scale=-0.7)
         nc.scalar.activation(out=stay[:, 1:S + 1], in_=haz_ps[:], func=ACT.Copy, scale=-100.0, bias=100.0)
-        start_sb = over.tile([P, S], F32, name="start_sb", offset=START_AT)
+        start_sb = keep.tile([P, S], F32, name="start_sb")
         start_sum = keep.tile([P, 1], F32, name="start_sum")
         nc.scalar.activation(out=start_sb[:], in_=start_ps[:], func=ACT.Copy, accum_out=start_sum[:])
         excess = keep.tile([P, 1], F32, name="excess")
@@ -248,7 +246,7 @@ def tile_picked_ybocpd_post_p_kernel(tc, x_words, x_scales, hT, norm, post, haz,
                 for b in range(NB):
                     load_post(b, POST_AT + b * ROW_BYTES if b else RAW0_AT + ROW_BYTES)
                 cast_h(0, 1, 0, nc.vector.tensor_copy, X1_AT)
-                cast_h(0, 1, 1, nc.scalar.copy, START_AT - LAP)
+                cast_h(0, 1, 1, nc.vector.tensor_copy, X1_AT + HALF_ROW)
             for half in range(2):
                 quant_h(0, g, half)
             for jb in range(NB):

@@ -30,11 +30,13 @@ WIN_BYTES = T * 4
 LAP = 512
 SCALE_AT = RAW_BYTES - LAP
 PICK0_AT = SCALE_AT + T - LAP
-CAST0_AT = PICK0_AT + ROW_BYTES
-X0_AT = CAST0_AT + ROW_BYTES - LAP
-X1_AT = X0_AT + LAP + 2 * RAW_BYTES
-POST_AT = X1_AT + HALF_ROW
-RAW0_AT = POST_AT + NB * ROW_BYTES
+THIRD_AT = PICK0_AT + ROW_BYTES
+X0_AT = THIRD_AT + ROW_BYTES
+PICK1_AT = THIRD_AT + RAW_BYTES
+POST0_AT = PICK1_AT + ROW_BYTES
+LAST_AT = POST0_AT + ROW_BYTES
+X1_AT = LAST_AT + RAW_BYTES
+RAW0_AT = X1_AT + WIN_BYTES
 DENS_AT = RAW0_AT + RAW_BYTES + HALF_ROW
 
 
@@ -77,8 +79,8 @@ def tile_picked_ybocpd_post_p_kernel(tc, x_words, x_scales, hT, norm, post, haz,
         hs_rows = keep.tile([P, P], F32, name="hs_rows")
         nc.scalar.dma_start(out=hs_rows[HS_ROW:HS_ROW + NB, :], in_=haz[0:1, :].rearrange("r (b p) -> (r b) p", p=P))
         nc.scalar.dma_start(out=hs_rows[HS_ROW + NB:P, :], in_=start[0:1, :].rearrange("r (b p) -> (r b) p", p=P))
-        load_h(0, 0, over.tile([P, 4, W], F32, name="h_raw00", offset=RAW0_AT))
         load_x(1, over.tile([P, T], I32, name="x_win1", offset=X1_AT))
+        load_h(0, 0, over.tile([P, 4, W], F32, name="h_raw00", offset=RAW0_AT))
 
         joint = {}
         for b in range(NB):
@@ -111,8 +113,12 @@ def tile_picked_ybocpd_post_p_kernel(tc, x_words, x_scales, hT, norm, post, haz,
             nc.vector.tensor_copy(x_pick[g][:], x_win[g][:].bitcast(U32).indirect(offsets[:]))
 
         pick_x(0, PICK0_AT)
-        for g in range(PASSES):
-            load_h(1, g, over.tile([P, 4, W], F32, name="h_raw1%d" % g, offset=X0_AT + LAP + g * RAW_BYTES))
+        for g, at in enumerate((THIRD_AT, LAST_AT)):
+            load_h(1, g, over.tile([P, 4, W], F32, name="h_raw1%d" % g, offset=at))
+        load_post(0, POST0_AT)
+        pick_x(1, PICK1_AT)
+        for b in range(1, NB):
+            load_post(b, X1_AT + b * ROW_BYTES)
 
         n_pick = keep.tile([P, S], F32, name="n_pick")
         nc.scalar.activation(out=n_pick[:], in_=n_win[:].indirect(offsets[:]), func=ACT.Copy)
@@ -202,7 +208,7 @@ def tile_picked_ybocpd_post_p_kernel(tc, x_words, x_scales, hT, norm, post, haz,
 
         def grow(b):
             if b == 0:
-                grown[b] = over.tile([P, S], F32, name="grown0", offset=X0_AT + LAP + HALF_ROW)
+                grown[b] = over.tile([P, S], F32, name="grown0", offset=THIRD_AT + HALF_ROW)
             else:
                 grown[b] = keep.tile([P, S], F32, name="grown%d" % b)
             nc.gpsimd.tensor_tensor(out=grown[b][:], in0=joint[b][:, 0:S], in1=stay[:, 0:S], op=ALU.mult)
@@ -237,23 +243,16 @@ def tile_picked_ybocpd_post_p_kernel(tc, x_words, x_scales, hT, norm, post, haz,
         whole = ((slice(0, S), nc.sync),)
         halves = ((slice(0, S // 2), nc.sync), (slice(S // 2, S), nc.scalar))
 
-        for g in range(PASSES):
-            if g == 0:
-                cast_h(0, 0, 1, nc.vector.tensor_copy, CAST0_AT + HALF_ROW)
-                cast_h(0, 0, 0, nc.vector.tensor_copy, SCALE_AT + LAP)
-            else:
-                pick_x(1, RAW0_AT)
-                for b in range(NB):
-                    load_post(b, POST_AT + b * ROW_BYTES if b else RAW0_AT + ROW_BYTES)
-                cast_h(0, 1, 0, nc.vector.tensor_copy, X1_AT)
-                cast_h(0, 1, 1, nc.vector.tensor_copy, X1_AT + HALF_ROW)
+        for g, at in enumerate((X1_AT, RAW0_AT)):
+            for half in range(2):
+                cast_h(0, g, half, nc.vector.tensor_copy, at + half * HALF_ROW)
             for half in range(2):
                 quant_h(0, g, half)
             for jb in range(NB):
                 mx_pass(0, g, jb)
         for jb in range(NB):
             exp_of(0, jb, 0, W if jb < 2 else P)
-        for g, at in enumerate((0, X0_AT + LAP)):
+        for g, at in enumerate((0, THIRD_AT)):
             for half in range(2):
                 cast_h(1, g, half, nc.vector.tensor_copy, at + half * HALF_ROW)
             quant_h(1, g, 0)

@@ -241,7 +241,7 @@ def tile_picked_ybocpd_post_p_kernel(tc, x_words, x_scales, hT, norm, post, haz,
                 queue.dma_start(out=out[b * P:(b + 1) * P, cols], in_=res[:, cols])
 
         whole = ((slice(0, S), nc.sync),)
-        halves = ((slice(0, S // 2), nc.sync), (slice(S // 2, S), nc.scalar))
+        halves = ((slice(0, S // 2), nc.sync), (slice(S // 2, S), nc.sync))
 
         for g, at in enumerate((X1_AT, RAW0_AT)):
             for half in range(2):

from contextlib import ExitStack

import concourse.mybir as mybir
from concourse.masks import make_identity

K, T, S, V = 1024, 2048, 512, 512
P = 128
PASSES = 2
NB = 4
FLOPS = 2 * K * S * V

F32 = mybir.dt.float32
BF16 = mybir.dt.bfloat16
I32 = mybir.dt.int32
U32 = mybir.dt.uint32
U16 = mybir.dt.uint16
U8 = mybir.dt.uint8
FP8X4 = mybir.dt.float8_e4m3fn_x4
ALU = mybir.AluOpType
ACT = mybir.ActivationFunctionType

W = 256
PARK = 96
NORM_ROW = P - 1
HS_ROW = P - 2 * NB
RAW_BYTES = 4 * W * 4
ROW_BYTES = S * 4
HALF_ROW = ROW_BYTES // 2
WIN_BYTES = T * 4
LAP = 512
SCALE_AT = RAW_BYTES - LAP
PICK0_AT = SCALE_AT + T - LAP
THIRD_AT = PICK0_AT + ROW_BYTES
X0_AT = THIRD_AT + ROW_BYTES
PICK1_AT = THIRD_AT + RAW_BYTES
POST0_AT = PICK1_AT + ROW_BYTES
LAST_AT = POST0_AT + ROW_BYTES
X1_AT = LAST_AT + RAW_BYTES
RAW0_AT = X1_AT + WIN_BYTES
DENS_AT = RAW0_AT + RAW_BYTES + HALF_ROW


def tile_picked_ybocpd_post_p_kernel(tc, x_words, x_scales, hT, norm, post, haz, start, offs, out):
    nc = tc.nc
    with ExitStack() as ctx:
        keep = ctx.enter_context(tc.tile_pool(name="keep", bufs=1))
        over = ctx.enter_context(tc.tile_pool(name="over", bufs=1))
        psum = ctx.enter_context(tc.psum_pool(name="psum", bufs=1))

        def h_rows(c, g):
            return hT[512 * g:512 * (g + 1), c * W:(c + 1) * W].rearrange("(p j) w -> p j w", j=4)

        h_raw = {}

        def load_h(c, g, tile):
            h_raw[c, g] = tile
            nc.sync.dma_start(out=tile[:], in_=h_rows(c, g))

        x_win = {}

        def load_x(g, tile):
            x_win[g] = tile
            nc.sync.dma_start(out=tile[:], in_=x_words[g].rearrange("p n t -> p (n t)").bitcast(I32))

        post_sb = {}

        def load_post(b, at):
            post_sb[b] = over.tile([P, S], F32, name="post%d" % b, offset=at)
            nc.sync.dma_start(out=post_sb[b][:], in_=post[b * P:(b + 1) * P, :])

        offsets = keep.tile([P, S // 16], U16, name="offsets")
        nc.sync.dma_start(offsets[:], offs)
        s_win = over.tile([P, T], U8, name="s_win", offset=SCALE_AT)
        nc.sync.dma_start(out=s_win[PARK:P, :].bitcast(I32),
                          in_=x_scales.bitcast(I32).rearrange("g m n -> m g n"))
        load_x(0, over.tile([P, T], I32, name="x_win0", offset=X0_AT))
        n_win = keep.tile([P, T], F32, name="n_win")
        nc.scalar.dma_start(out=n_win[NORM_ROW:P, :], in_=norm[0:1, :])
        hs_rows = keep.tile([P, P], F32, name="hs_rows")
        nc.scalar.dma_start(out=hs_rows[HS_ROW:HS_ROW + NB, :], in_=haz[0:1, :].rearrange("r (b p) -> (r b) p", p=P))
        nc.scalar.dma_start(out=hs_rows[HS_ROW + NB:P, :], in_=start[0:1, :].rearrange("r (b p) -> (r b) p", p=P))
        load_x(1, over.tile([P, T], I32, name="x_win1", offset=X1_AT))
        load_h(0, 0, over.tile([P, 4, W], F32, name="h_raw00", offset=RAW0_AT))

        joint = {}
        for b in range(NB):
            joint[b] = keep.tile([P, S + 1], F32, name="joint%d" % b)
        stay = keep.tile([P, S + 1], F32, name="stay")
        nc.gpsimd.memset(stay[:, 0:1], 0.0)
        one = keep.tile([P, 1], F32, name="one")
        nc.scalar.activation(out=one[:], in_=stay[:, 0:1], func=ACT.Exp)
        for b in range(NB):
            nc.gpsimd.memset(joint[b][:, 0:1], 0.0)
        nc.vector.memset(s_win[0:PARK, :].bitcast(I32), 0)
        nc.vector.memset(n_win[0:NORM_ROW, :], 0.0)
        s_plane = keep.tile([P, PASSES * S], U8, name="s_plane", align_bytes=64)
        nc.gpsimd.memset(s_plane[:].bitcast(I32), 0)
        nc.gpsimd.memset(hs_rows[0:HS_ROW, :], 0.0)
        ident = keep.tile([P, P], F32, name="ident")
        make_identity(nc, ident[:])

        s_pick = keep.tile([P, S], U8, name="s_pick", align_bytes=64)
        nc.vector.tensor_copy(s_pick[:], s_win[:].indirect(offsets[:]))
        for q in range(4):
            nc.sync.dma_start(out=s_plane[32 * q:32 * q + 4, :].bitcast(I32).rearrange("r (g n) -> r g n", g=PASSES),
                                in_=s_pick[PARK + 8 * q:PARK + 8 * q + 8, :].bitcast(I32))
        load_h(0, 1, over.tile([P, 4, W], F32, name="h_raw01", offset=0))

        x_pick = {}

        def pick_x(g, at):
            x_pick[g] = over.tile([P, S], U32, name="x_pick%d" % g, align_bytes=64, offset=at)
            nc.vector.tensor_copy(x_pick[g][:], x_win[g][:].bitcast(U32).indirect(offsets[:]))

        pick_x(0, PICK0_AT)
        for g, at in enumerate((THIRD_AT, LAST_AT)):
            load_h(1, g, over.tile([P, 4, W], F32, name="h_raw1%d" % g, offset=at))
        load_post(0, POST0_AT)
        pick_x(1, PICK1_AT)
        for b in range(1, NB):
            load_post(b, X1_AT + b * ROW_BYTES)

        n_pick = keep.tile([P, S], F32, name="n_pick")
        nc.scalar.activation(out=n_pick[:], in_=n_win[:].indirect(offsets[:]), func=ACT.Copy)

        h_bf, h_quant = {}, {}

        def cast_h(c, g, half, copy, at):
            tile = over.tile([P, P, 4], BF16, name="h_bf%d%d%d" % (c, g, half), align_bytes=64, offset=at)
            h_bf[c, g, half] = tile
            copy(out=tile[:].rearrange("p (c i) t -> p c t i", i=4),
                 in_=h_raw[c, g][:, :, half * P:(half + 1) * P].rearrange("p t (c i) -> p c t i", i=4))

        def quant_h(c, g, half):
            if half == 0:
                h_quant[c, g] = (keep.tile([P, W], U32, name="h_codes%d%d" % (c, g), align_bytes=64),
                                 keep.tile([P, W], U8, name="h_scales%d%d" % (c, g), align_bytes=64))
            codes, scales = h_quant[c, g]
            cols = slice(half * P, (half + 1) * P)
            nc.vector.quantize_mx(out=codes[:, cols].bitcast(FP8X4), scales=scales[:, cols],
                                  in_=h_bf[c, g, half][:].rearrange("p w j -> p (w j)"))

        is_last = ident[:, P - 1:P]
        not_last = keep.tile([P, 1], F32, name="not_last")
        nc.scalar.activation(out=not_last[:], in_=is_last, func=ACT.Identity, scale=-1.0, bias=one[:])
        hs_ps = psum.tile([P, 2, P], F32, name="hs_ps", tag="turn", bufs=2)
        nc.tensor.transpose(hs_ps[:, 0, :], hs_rows[:], ident[:])
        nc.tensor.transpose(hs_ps[:, 1, :], hs_rows[:, P - 1:P].to_broadcast([P, P]), ident[:])
        hs_cols = keep.tile([P, 2 * NB], F32, name="hs_cols")
        last_haz = HS_ROW + NB - 1
        nc.scalar.copy(out=hs_cols[:, 0:NB - 1], in_=hs_ps[:, 0, HS_ROW:last_haz])
        nc.scalar.activation(out=hs_cols[:, NB - 1:NB], in_=hs_ps[:, 0, last_haz:last_haz + 1], func=ACT.Identity,
                             scale=not_last[:], bias=is_last)
        nc.scalar.activation(out=hs_cols[:, NB:2 * NB], in_=hs_ps[:, 0, last_haz + 1:P], func=ACT.Copy, scale=100.0)
        haz_end = keep.tile([P, 1], F32, name="haz_end")
        nc.scalar.copy(out=haz_end[:], in_=hs_ps[:, 1, last_haz:last_haz + 1])
        haz_ps = psum.tile([P, S], F32, name="haz_ps")
        start_ps = psum.tile([P, S], F32, name="start_ps")
        for a, bank in enumerate((haz_ps, start_ps)):
            for jb in range(NB):
                col = a * NB + jb
                nc.tensor.transpose(bank[:, jb * P:(jb + 1) * P], hs_cols[:, col:col + 1].to_broadcast([P, P]), ident[:])
        n_ps = psum.tile([P, NB, P], F32, name="n_ps", tag="turn", bufs=2)
        for jb in range(NB):
            nc.tensor.transpose(n_ps[:, jb, :], n_pick[:, jb * P:(jb + 1) * P], ident[:])
        bias = keep.tile([P, NB], F32, name="bias")
        nc.scalar.activation(out=bias[:], in_=n_ps[:, :, NORM_ROW], func=ACT.Copy, scale=-0.7)
        nc.scalar.activation(out=stay[:, 1:S + 1], in_=haz_ps[:], func=ACT.Copy, scale=-100.0, bias=100.0)
        start_sb = keep.tile([P, S], F32, name="start_sb")
        start_sum = keep.tile([P, 1], F32, name="start_sum")
        nc.scalar.activation(out=start_sb[:], in_=start_ps[:], func=ACT.Copy, accum_out=start_sum[:])
        excess = keep.tile([P, 1], F32, name="excess")
        nc.scalar.activation(out=excess[:], in_=start_sum[:], func=ACT.Copy, scale=0.01, bias=-1.0)

        sums = {}

        def mx_pass(c, g, jb):
            if g == 0:
                sums[c, jb] = psum.tile([P, W], F32, name="sums%d%d" % (c, jb), tag="sums%d" % jb)
            codes, scales = h_quant[c, g]
            nc.tensor.matmul_mx(out=sums[c, jb][:], lhsT=x_pick[g][:, jb * P:(jb + 1) * P].bitcast(FP8X4),
                                lhsT_scale=s_plane[:, g * S + jb * P:g * S + (jb + 1) * P],
                                rhs=codes[:].bitcast(FP8X4), rhs_scale=scales[:],
                                start=(g == 0), stop=(g == PASSES - 1))

        dens = (keep.tile([P, NB, W], F32, name="dens0"), over.tile([P, NB, W], F32, name="dens1", offset=DENS_AT))

        def exp_of(c, jb, lo, hi):
            nc.scalar.activation(out=dens[c][:, jb, lo:hi], in_=sums[c, jb][:, lo:hi], func=ACT.Exp,
                                 bias=bias[:, jb:jb + 1], scale=0.7)

        grown, sums_v, sums_s, scaled = {}, {}, {}, {}

        def fold_end(b):
            last = post_sb[b][:, S - 1:S]
            if b == 0:
                nc.vector.tensor_scalar(last, last, haz_end[:], None, ALU.mult)
            else:
                nc.scalar.activation(out=last, in_=last, func=ACT.Copy, scale=haz_end[:])

        def turn(b):
            e_ps = psum.tile([P, S], F32, name="e_ps%d" % b, tag="turn", bufs=2)
            for jb in range(NB):
                nc.tensor.transpose(e_ps[:, jb * P:(jb + 1) * P], dens[b // 2][:, jb, (b % 2) * P:(b % 2 + 1) * P], ident[:])
            sums_v[b] = keep.tile([P, 3], F32, name="sums_v%d" % b)
            nc.vector.scalar_tensor_tensor(out=joint[b][:, 1:S + 1], in0=e_ps[:], scalar=1.0, in1=post_sb[b][:],
                                           op0=ALU.mult, op1=ALU.mult, accum_out=sums_v[b][:, 0:1])

        def grow(b):
            if b == 0:
                grown[b] = over.tile([P, S], F32, name="grown0", offset=THIRD_AT + HALF_ROW)
            else:
                grown[b] = keep.tile([P, S], F32, name="grown%d" % b)
            nc.gpsimd.tensor_tensor(out=grown[b][:], in0=joint[b][:, 0:S], in1=stay[:, 0:S], op=ALU.mult)

        def change(b):
            if b == 2:
                ch = over.tile([P, S], F32, name="ch2", offset=DENS_AT - HALF_ROW)
            else:
                ch = keep.tile([P, S], F32, name="ch%d" % b)
            nc.vector.scalar_tensor_tensor(out=ch[:], in0=haz_ps[:], scalar=1.0, in1=joint[b][:, 1:S + 1],
                                           op0=ALU.mult, op1=ALU.mult, accum_out=sums_v[b][:, 1:2])
            sums_s[b] = keep.tile([P, 2], F32, name="sums_s%d" % b)
            nc.scalar.activation(out=sums_s[b][:, 0:1], in_=sums_v[b][:, 1:2], func=ACT.Identity,
                                 scale=excess[:], bias=sums_v[b][:, 0:1])

        def invert(b):
            nc.vector.reciprocal(out=sums_v[b][:, 2:3], in_=sums_s[b][:, 0:1])
            nc.scalar.activation(out=sums_s[b][:, 1:2], in_=sums_v[b][:, 1:2], func=ACT.Copy, scale=sums_v[b][:, 2:3])
            scaled[b] = keep.tile([P, S], F32, name="scaled%d" % b)
            nc.scalar.activation(out=scaled[b][:], in_=grown[b][:], func=ACT.Copy, scale=sums_v[b][:, 2:3])

        def finish(b, pieces):
            if b < 2:
                res = over.tile([P, S], F32, name="res%d" % b, offset=DENS_AT + HALF_ROW + b * ROW_BYTES)
            else:
                res = keep.tile([P, S], F32, name="res%d" % b)
            for cols, queue in pieces:
                nc.vector.scalar_tensor_tensor(out=res[:, cols], in0=start_ps[:, cols], scalar=sums_s[b][:, 1:2],
                                               in1=scaled[b][:, cols], op0=ALU.mult, op1=ALU.add)
                queue.dma_start(out=out[b * P:(b + 1) * P, cols], in_=res[:, cols])

        whole = ((slice(0, S), nc.sync),)
        halves = ((slice(0, S // 2), nc.sync), (slice(S // 2, S), nc.sync))

        for g, at in enumerate((X1_AT, RAW0_AT)):
            for half in range(2):
                cast_h(0, g, half, nc.vector.tensor_copy, at + half * HALF_ROW)
            for half in range(2):
                quant_h(0, g, half)
            for jb in range(NB):
                mx_pass(0, g, jb)
        for jb in range(NB):
            exp_of(0, jb, 0, W if jb < 2 else P)
        for g, at in enumerate((0, THIRD_AT)):
            for half in range(2):
                cast_h(1, g, half, nc.vector.tensor_copy, at + half * HALF_ROW)
            quant_h(1, g, 0)
            if g == 1:
                fold_end(0)
            quant_h(1, g, 1)
        turn(0)
        grow(0)
        for jb in (2, 3):
            exp_of(0, jb, P, W)
        for b in range(1, NB):
            fold_end(b)
        turn(1)
        grow(1)
        for g in range(PASSES):
            for jb in range(NB):
                mx_pass(1, g, jb)
        for jb in range(NB):
            exp_of(1, jb, 0, W if jb < 2 else P)
        change(0)
        change(1)
        invert(0)
        turn(2)
        grow(2)
        for jb in (2, 3):
            exp_of(1, jb, P, W)
        invert(1)
        turn(3)
        grow(3)
        change(2)
        change(3)
        invert(2)
        finish(0, whole)
        invert(3)
        finish(1, whole)
        finish(2, whole)
        finish(3, halves)
